import numpy as np
import ml_dtypes


def mxq(x, axis, fmt="e4m3"):
    dtype, down = {"e4m3": (ml_dtypes.float8_e4m3fn, 7), "e5m2": (ml_dtypes.float8_e5m2, 14)}[fmt]
    v = np.moveaxis(np.asarray(x, np.float32).astype(ml_dtypes.bfloat16).astype(np.float64), axis, -1)
    blocks = v.reshape(v.shape[:-1] + (-1, 32))
    amax = np.abs(blocks).max(-1, keepdims=True)
    byte = np.maximum(np.where(amax > 0, np.frexp(amax)[1] - 1 + 127, 0) - down, 1)
    scale = np.exp2(byte - 127.0)
    codes = (blocks / scale).astype(np.float32).astype(dtype).astype(np.float64)
    return np.moveaxis((codes * scale).reshape(v.shape), -1, axis)


WIDE = False


def mx_kscale(k):
    if not WIDE:
        return np.ones(k)
    levels = np.array([10, -10, 5, -5, 0])
    if k % 512:
        return np.exp2(np.random.permutation(np.resize(levels, k // 32))).repeat(32)
    a = np.empty((k // 512, 16))
    for p in range(k // 512):
        a[p, :8] = np.random.permutation(np.resize(levels, 8))
        for g in range(8):
            far = levels[np.abs(levels - a[p, g]) >= 10]
            a[p, g + 8] = far[np.random.randint(len(far))]
    return np.exp2(a.ravel()).repeat(32)


def f64(x):
    return np.asarray(x).astype(np.float64)


def striped(idx):
    return np.tile(idx.reshape(-1, 16).T, (8, 1)).astype(np.uint16)


def unstriped(offs):
    return offs[:16].T.reshape(-1).astype(np.int64)


E2M1 = np.array([0.0, 0.5, 1.0, 1.5, 2.0, 3.0, 4.0, 6.0, -0.0, -0.5, -1.0, -1.5, -2.0, -3.0, -4.0, -6.0])


def pack_fp4(w):
    k, n = w.shape
    w = f64(np.asarray(w, np.float32).astype(ml_dtypes.bfloat16)).reshape(k // 32, 32, n)
    amax = np.abs(w).max(1)
    mant, ex = np.frexp(amax / 6.0)
    byte = np.clip(np.where(amax > 0, np.where(mant > 0.5, ex, ex - 1) + 127, 1), 1, 254)
    scaled = (w * np.exp2(127.0 - byte)[:, None, :]).reshape(k, n).astype(np.float32)
    c = np.ascontiguousarray(scaled.reshape(k // 512, 128, 4, n).transpose(0, 1, 3, 2)).astype(ml_dtypes.float4_e2m1fn).view(np.uint8) & 0xF
    words = (c[..., 0::2] | (c[..., 1::2] << 4)).reshape(k // 512, 128, 2 * n)
    return np.ascontiguousarray(words), np.ascontiguousarray(byte.astype(np.uint8).reshape(k // 512, 16, n))


def unpack_fp4(words, scales):
    g, _, n = scales.shape
    words = np.ascontiguousarray(words).reshape(g, 128, n, 2)
    nib = np.empty((g, 128, n, 4), np.uint8)
    nib[..., 0::2] = words & 0xF
    nib[..., 1::2] = words >> 4
    vals = E2M1[nib] * np.repeat(np.exp2(scales.astype(np.float64) - 127.0), 8, axis=1)[..., None]
    return vals.transpose(0, 1, 3, 2).reshape(g * 512, n)


def gelu(v):
    return 0.5 * v * (1.0 + np.tanh(np.sqrt(2.0 / np.pi) * (v + 0.044715 * v**3)))


K, T, S, H, N = 512, 2048, 1024, 512, 128
P = 2 ** 7


def setup_inputs():
    n = np.random.standard_normal
    s = mx_kscale(K)[:, None]
    u = mx_kscale(H)
    packed_w2 = pack_fp4(n((H, N)) / np.sqrt(H) / u[:, None])
    return {
        "xT": (n((K, T)) * s).astype(np.float32),
        "gate": np.tile(np.random.uniform(0.2, 1.0, S), (P, 1)).astype(np.float32),
        "res": n((N, T)).astype(np.float32),
        "w1": (n((K, H)) / np.sqrt(K) / s * u).astype(np.float32),
        "w2_words": packed_w2[0],
        "w2_scales": packed_w2[1],
        "offs": striped(np.random.permutation(T)[:S]),
    }


def reference(xT, gate, res, w1, w2_words, w2_scales, offs):
    r = f64(res)[:, unstriped(offs)]
    xq = mxq(f64(xT)[:, unstriped(offs)], 0, "e4m3")
    h = gelu(mxq(f64(w1), 0, "e4m3").T @ xq)
    y = unpack_fp4(w2_words, w2_scales).T @ mxq(h, 0, "e4m3")
    out = f64(res).copy()
    out[:, unstriped(offs)] = r + y * f64(gate)[:1]
    return out

@@ -1,0 +1,146 @@
+from contextlib import ExitStack
+
+import concourse.mybir as mybir
+
+K, T, S, H, N = 512, 2048, 1024, 512, 128
+FLOPS = 2 * K * H * S + 2 * H * N * S
+
+F32 = mybir.dt.float32
+BF16 = mybir.dt.bfloat16
+I32 = mybir.dt.int32
+U32 = mybir.dt.uint32
+U16 = mybir.dt.uint16
+U8 = mybir.dt.uint8
+FP8X4 = mybir.dt.float8_e4m3fn_x4
+FP4X4 = mybir.dt.float4_e2m1fn_x4
+GELU = mybir.ActivationFunctionType.Gelu_apprx_tanh
+MULT = mybir.AluOpType.mult
+ADD = mybir.AluOpType.add
+
+P = 128
+PACK = 4
+CHUNK = 256
+CHUNKS = S // CHUNK
+COLS = CHUNK // 16
+SUB = 128
+
+LOADS_A = ((0, 1024, 1024), (1024, 1024, 704))
+LOADS_B = ((0, 512, 0), (512, 512, 0), (1024, 512, 0), (1536, 512, 352))
+
+
+def tile_picked_modres_mlpgelu_l_kernel(tc, xT, gate, res, w1, w2_words, w2_scales, offs, out):
+    nc = tc.nc
+    with ExitStack() as ctx:
+        keep = ctx.enter_context(tc.tile_pool(name="keep", bufs=1))
+        psum1 = ctx.enter_context(tc.psum_pool(name="psum1", bufs=6))
+        psum2 = ctx.enter_context(tc.psum_pool(name="psum2", bufs=2))
+
+        offsets = keep.tile([P, S // 16], U16, name="offsets")
+        x_rows = xT.rearrange("(p j) t -> p j t", j=PACK)
+        w1_rows = w1.rearrange("(p j) c -> p j c", j=PACK)
+
+        zero = keep.tile([P, 1], F32, name="zero")
+        zero_bias = keep.tile([P, 1], F32, name="zero_bias")
+        nc.vector.memset(zero[:], 0.0)
+        nc.scalar.activation(out=zero_bias[:], in_=zero[:], func=GELU)
+
+        w2_codes = keep.tile([P, 2 * N], U8, name="w2_codes", align_bytes=64)
+        w2_plane = keep.tile([P, N], U8, name="w2_plane", align_bytes=64)
+        nc.gpsimd.memset(w2_plane[:].bitcast(I32), 0)
+        nc.gpsimd.dma_start(out=w2_codes[:].bitcast(I32), in_=w2_words[0].bitcast(I32))
+        for q in range(4):
+            nc.gpsimd.dma_start(out=w2_plane[32 * q : 32 * q + 4, :].bitcast(I32), in_=w2_scales[0, 4 * q : 4 * q + 4, :].bitcast(I32))
+
+        pairs = [keep.tile([P, T, 2], BF16, name="pairs%d" % u) for u in range(2)]
+        raw = {}
+        for u, loads in enumerate((LOADS_A, LOADS_B)):
+            for first, count, share in loads:
+                raw[u, first] = keep.tile([P, 2, count], F32, name="raw%d_%d" % (u, first))
+                nc.sync.dma_start(out=raw[u, first][:], in_=x_rows[:, 2 * u : 2 * u + 2, first : first + count])
+                if (u, first) == (0, 0):
+                    nc.sync.dma_start(offsets[:], offs)
+        w1_raw = [keep.tile([P, PACK, H // 2], F32, name="w1_raw%d" % v) for v in range(2)]
+        for v in range(2):
+            nc.sync.dma_start(out=w1_raw[v][:], in_=w1_rows[:, :, v * (H // 2) : (v + 1) * (H // 2)])
+        window = keep.tile([P, T], F32, name="window")
+        nc.sync.dma_start(out=window[:], in_=res)
+        gates = keep.tile([P, S], F32, name="gates")
+        nc.sync.dma_start(out=gates[:], in_=gate)
+
+        def cast(u):
+            for first, count, share in (LOADS_A, LOADS_B)[u]:
+                src = raw[u, first][:].rearrange("p j t -> p t j")
+                if share > 0:
+                    nc.vector.tensor_copy(out=pairs[u][:, first : first + share, :], in_=src[:, 0:share, :])
+                if share < count:
+                    nc.scalar.copy(out=pairs[u][:, first + share : first + count, :], in_=src[:, share:count, :])
+
+        picked = [keep.tile([P, CHUNK, 2], U32, name="picked%d" % c, align_bytes=64) for c in range(CHUNKS)]
+
+        def gather(u, c):
+            words = pairs[u][:].rearrange("p t j -> p (t j)").bitcast(U32)
+            nc.vector.tensor_copy(out=picked[c][:, :, u], in_=words.indirect(offsets[:, c * COLS : (c + 1) * COLS]))
+
+        x_codes = [keep.tile([P, CHUNK], U32, name="x_codes%d" % c, align_bytes=64) for c in range(CHUNKS)]
+        x_plane = [keep.tile([P, CHUNK], U8, name="x_plane%d" % c, align_bytes=64) for c in range(CHUNKS)]
+
+        def quantize_x(c):
+            nc.vector.quantize_mx(out=x_codes[c][:].bitcast(FP8X4), scales=x_plane[c][:], in_=picked[c][:].rearrange("p s u -> p (s u)").bitcast(BF16))
+
+        cast(0)
+        for c in range(CHUNKS):
+            gather(0, c)
+        cast(1)
+
+        w1_grouped = keep.tile([P, PACK, P, PACK], BF16, name="w1_grouped", align_bytes=64)
+        w1_codes = keep.tile([P, H], U32, name="w1_codes", align_bytes=64)
+        w1_plane = keep.tile([P, H], U8, name="w1_plane", align_bytes=64)
+        for v in range(2):
+            nc.scalar.copy(
+                out=w1_grouped[:, :, v * 64 : (v + 1) * 64, :].rearrange("p t m j -> p m t j"),
+                in_=w1_raw[v][:].rearrange("p j (m t) -> p m t j", t=PACK),
+            )
+        nc.vector.quantize_mx(out=w1_codes[:].bitcast(FP8X4), scales=w1_plane[:], in_=w1_grouped[:].rearrange("p t m j -> p (t m j)"))
+
+        gather(1, 0)
+        for c in range(CHUNKS):
+            if c + 1 < CHUNKS:
+                gather(1, c + 1)
+            quantize_x(c)
+
+        kept = keep.tile([P, S], F32, name="kept")
+        gated = keep.tile([P, S], F32, name="gated")
+        for c in range(CHUNKS):
+            cols = slice(c * CHUNK, (c + 1) * CHUNK)
+            hidden = keep.tile([P, CHUNK, PACK], BF16, name="hidden%d" % c, align_bytes=64)
+            for b in range(CHUNK // SUB):
+                sub = slice(b * SUB, (b + 1) * SUB)
+                pre = psum1.tile([P, PACK, SUB], F32, name="pre")
+                for t in range(PACK):
+                    nc.tensor.matmul_mx(
+                        out=pre[:, t, :],
+                        lhsT=w1_codes[:, t * P : (t + 1) * P].bitcast(FP8X4),
+                        lhsT_scale=w1_plane[:, t * P : (t + 1) * P],
+                        rhs=x_codes[c][:, sub].bitcast(FP8X4),
+                        rhs_scale=x_plane[c][:, sub],
+                        start=True,
+                        stop=True,
+                    )
+                nc.scalar.activation(out=hidden[:, sub, :], in_=pre[:].rearrange("p t n -> p n t"), func=GELU, bias=zero_bias[:])
+            h_codes = keep.tile([P, CHUNK], U32, name="h_codes%d" % c, align_bytes=64)
+            h_plane = keep.tile([P, CHUNK], U8, name="h_plane%d" % c, align_bytes=64)
+            nc.vector.quantize_mx(out=h_codes[:].bitcast(FP8X4), scales=h_plane[:], in_=hidden[:].rearrange("p s t -> p (s t)"))
+            nc.vector.tensor_copy(out=kept[:, cols], in_=window[:].indirect(offsets[:, c * COLS : (c + 1) * COLS]))
+            y = psum2.tile([P, CHUNK], F32, name="y")
+            nc.tensor.matmul_mx(
+                out=y[:],
+                lhsT=w2_codes[:].bitcast(FP4X4),
+                lhsT_scale=w2_plane[:],
+                rhs=h_codes[:].bitcast(FP8X4),
+                rhs_scale=h_plane[:],
+                start=True,
+                stop=True,
+            )
+            nc.vector.tensor_tensor(out=gated[:, cols], in0=y[:], in1=gates[:, cols], op=MULT)
+        nc.vector.tensor_tensor(window[:].indirect(offsets[:]), kept[:], gated[:], ADD)
+        nc.sync.dma_start(out=out, in_=window[:])

@@ -1,6 +1,7 @@
 from contextlib import ExitStack
 
 import concourse.mybir as mybir
+from concourse.masks import make_identity
 
 K, T, S, H, N = 512, 2048, 1024, 512, 128
 FLOPS = 2 * K * H * S + 2 * H * N * S
@@ -14,28 +15,33 @@ U8 = mybir.dt.uint8
 FP8X4 = mybir.dt.float8_e4m3fn_x4
 FP4X4 = mybir.dt.float4_e2m1fn_x4
 GELU = mybir.ActivationFunctionType.Gelu_apprx_tanh
-MULT = mybir.AluOpType.mult
+COPY = mybir.ActivationFunctionType.Copy
 ADD = mybir.AluOpType.add
 
 P = 128
 PACK = 4
 CHUNK = 256
 CHUNKS = S // CHUNK
-COLS = CHUNK // 16
 SUB = 128
+LATER = S - CHUNK
 
-LOADS_A = ((0, 1024, 1024), (1024, 1024, 704))
-LOADS_B = ((0, 512, 0), (512, 512, 0), (1024, 512, 0), (1536, 512, 352))
+LOADS_A = ((0, 1024, 512), (1024, 1024, 608))
+LOADS_B = ((0, 512, 0), (512, 512, 0), (1024, 512, 0), (1536, 512, 320))
 
 
 def tile_picked_modres_mlpgelu_l_kernel(tc, xT, gate, res, w1, w2_words, w2_scales, offs, out):
     nc = tc.nc
     with ExitStack() as ctx:
         keep = ctx.enter_context(tc.tile_pool(name="keep", bufs=1))
-        psum1 = ctx.enter_context(tc.psum_pool(name="psum1", bufs=6))
-        psum2 = ctx.enter_context(tc.psum_pool(name="psum2", bufs=2))
+        psum1 = ctx.enter_context(tc.psum_pool(name="psum1", bufs=5))
+        psum2 = ctx.enter_context(tc.psum_pool(name="psum2", bufs=1))
+        psum3 = ctx.enter_context(tc.psum_pool(name="psum3", bufs=2))
 
         offsets = keep.tile([P, S // 16], U16, name="offsets")
+
+        def entries(first, count):
+            return offsets[:, first // 16 : (first + count) // 16]
+
         x_rows = xT.rearrange("(p j) t -> p j t", j=PACK)
         w1_rows = w1.rearrange("(p j) c -> p j c", j=PACK)
 
@@ -51,6 +57,9 @@ def tile_picked_modres_mlpgelu_l_kernel(tc, xT, gate, res, w1, w2_words, w2_scal
         for q in range(4):
             nc.gpsimd.dma_start(out=w2_plane[32 * q : 32 * q + 4, :].bitcast(I32), in_=w2_scales[0, 4 * q : 4 * q + 4, :].bitcast(I32))
 
+        identity = keep.tile([P, P], F32, name="identity")
+        make_identity(nc, identity[:])
+
         pairs = [keep.tile([P, T, 2], BF16, name="pairs%d" % u) for u in range(2)]
         raw = {}
         for u, loads in enumerate((LOADS_A, LOADS_B)):
@@ -59,13 +68,14 @@ def tile_picked_modres_mlpgelu_l_kernel(tc, xT, gate, res, w1, w2_words, w2_scal
                 nc.sync.dma_start(out=raw[u, first][:], in_=x_rows[:, 2 * u : 2 * u + 2, first : first + count])
                 if (u, first) == (0, 0):
                     nc.sync.dma_start(offsets[:], offs)
-        w1_raw = [keep.tile([P, PACK, H // 2], F32, name="w1_raw%d" % v) for v in range(2)]
+        w1_raw = [keep.tile([P, PACK, H // 2], F32, name="w1_raw%d" % v, tag="w1_raw%d" % v, align_bytes=64) for v in range(2)]
         for v in range(2):
             nc.sync.dma_start(out=w1_raw[v][:], in_=w1_rows[:, :, v * (H // 2) : (v + 1) * (H // 2)])
         window = keep.tile([P, T], F32, name="window")
         nc.sync.dma_start(out=window[:], in_=res)
-        gates = keep.tile([P, S], F32, name="gates")
-        nc.sync.dma_start(out=gates[:], in_=gate)
+        gate_cols = keep.tile([P, S // P], F32, name="gate_cols")
+        with nc.allow_non_contiguous_dma(reason="one gate value a partition"):
+            nc.sync.dma_start(out=gate_cols[:], in_=gate[0].rearrange("(b p) -> p b", p=P))
 
         def cast(u):
             for first, count, share in (LOADS_A, LOADS_B)[u]:
@@ -75,22 +85,24 @@ def tile_picked_modres_mlpgelu_l_kernel(tc, xT, gate, res, w1, w2_words, w2_scal
                 if share < count:
                     nc.scalar.copy(out=pairs[u][:, first + share : first + count, :], in_=src[:, share:count, :])
 
-        picked = [keep.tile([P, CHUNK, 2], U32, name="picked%d" % c, align_bytes=64) for c in range(CHUNKS)]
+        woven_first = keep.tile([P, CHUNK, 2], U32, name="woven_first", align_bytes=64)
+        apart = keep.tile([P, 2 * LATER], U32, name="apart")
 
-        def gather(u, c):
+        def gather(u):
             words = pairs[u][:].rearrange("p t j -> p (t j)").bitcast(U32)
-            nc.vector.tensor_copy(out=picked[c][:, :, u], in_=words.indirect(offsets[:, c * COLS : (c + 1) * COLS]))
+            nc.vector.tensor_copy(out=woven_first[:, :, u], in_=words.indirect(entries(0, CHUNK)))
+            nc.vector.tensor_copy(out=apart[:, u * LATER : (u + 1) * LATER], in_=words.indirect(entries(CHUNK, LATER)))
 
         x_codes = [keep.tile([P, CHUNK], U32, name="x_codes%d" % c, align_bytes=64) for c in range(CHUNKS)]
         x_plane = [keep.tile([P, CHUNK], U8, name="x_plane%d" % c, align_bytes=64) for c in range(CHUNKS)]
 
-        def quantize_x(c):
-            nc.vector.quantize_mx(out=x_codes[c][:].bitcast(FP8X4), scales=x_plane[c][:], in_=picked[c][:].rearrange("p s u -> p (s u)").bitcast(BF16))
+        def quantize_x(c, woven):
+            nc.vector.quantize_mx(out=x_codes[c][:].bitcast(FP8X4), scales=x_plane[c][:], in_=woven.bitcast(BF16))
 
-        cast(0)
-        for c in range(CHUNKS):
-            gather(0, c)
-        cast(1)
+        for u in range(2):
+            cast(u)
+            gather(u)
+        quantize_x(0, woven_first[:].rearrange("p s u -> p (s u)"))
 
         w1_grouped = keep.tile([P, PACK, P, PACK], BF16, name="w1_grouped", align_bytes=64)
         w1_codes = keep.tile([P, H], U32, name="w1_codes", align_bytes=64)
@@ -102,45 +114,88 @@ def tile_picked_modres_mlpgelu_l_kernel(tc, xT, gate, res, w1, w2_words, w2_scal
             )
         nc.vector.quantize_mx(out=w1_codes[:].bitcast(FP8X4), scales=w1_plane[:], in_=w1_grouped[:].rearrange("p t m j -> p (t m j)"))
 
-        gather(1, 0)
-        for c in range(CHUNKS):
-            if c + 1 < CHUNKS:
-                gather(1, c + 1)
-            quantize_x(c)
-
-        kept = keep.tile([P, S], F32, name="kept")
-        gated = keep.tile([P, S], F32, name="gated")
-        for c in range(CHUNKS):
-            cols = slice(c * CHUNK, (c + 1) * CHUNK)
-            hidden = keep.tile([P, CHUNK, PACK], BF16, name="hidden%d" % c, align_bytes=64)
-            for b in range(CHUNK // SUB):
-                sub = slice(b * SUB, (b + 1) * SUB)
-                pre = psum1.tile([P, PACK, SUB], F32, name="pre")
-                for t in range(PACK):
-                    nc.tensor.matmul_mx(
-                        out=pre[:, t, :],
-                        lhsT=w1_codes[:, t * P : (t + 1) * P].bitcast(FP8X4),
-                        lhsT_scale=w1_plane[:, t * P : (t + 1) * P],
-                        rhs=x_codes[c][:, sub].bitcast(FP8X4),
-                        rhs_scale=x_plane[c][:, sub],
-                        start=True,
-                        stop=True,
-                    )
-                nc.scalar.activation(out=hidden[:, sub, :], in_=pre[:].rearrange("p t n -> p n t"), func=GELU, bias=zero_bias[:])
-            h_codes = keep.tile([P, CHUNK], U32, name="h_codes%d" % c, align_bytes=64)
-            h_plane = keep.tile([P, CHUNK], U8, name="h_plane%d" % c, align_bytes=64)
-            nc.vector.quantize_mx(out=h_codes[:].bitcast(FP8X4), scales=h_plane[:], in_=hidden[:].rearrange("p s t -> p (s t)"))
-            nc.vector.tensor_copy(out=kept[:, cols], in_=window[:].indirect(offsets[:, c * COLS : (c + 1) * COLS]))
-            y = psum2.tile([P, CHUNK], F32, name="y")
-            nc.tensor.matmul_mx(
-                out=y[:],
-                lhsT=w2_codes[:].bitcast(FP4X4),
-                lhsT_scale=w2_plane[:],
-                rhs=h_codes[:].bitcast(FP8X4),
-                rhs_scale=h_plane[:],
-                start=True,
-                stop=True,
+        woven_later = keep.tile([P, 2 * LATER], U32, name="woven_later", tag="w1_raw1", align_bytes=64)
+        for c in range(1, CHUNKS):
+            woven = woven_later[:, 2 * (c - 1) * CHUNK : 2 * c * CHUNK]
+            nc.scalar.copy(
+                out=woven.rearrange("p (s u) -> p s u", u=2),
+                in_=apart[:].rearrange("p (u s) -> p s u", u=2)[:, (c - 1) * CHUNK : c * CHUNK, :],
             )
-            nc.vector.tensor_tensor(out=gated[:, cols], in0=y[:], in1=gates[:, cols], op=MULT)
-        nc.vector.tensor_tensor(window[:].indirect(offsets[:]), kept[:], gated[:], ADD)
+            quantize_x(c, woven)
+
+        half = S // 2
+        kept_first = keep.tile([P, half], F32, name="kept_first")
+        nc.vector.tensor_copy(out=kept_first[:], in_=window[:].indirect(entries(0, half)))
+        kept = [kept_first]
+
+        hidden, h_codes, h_plane, tall, rows, gated = {}, {}, {}, {}, {}, {}
+
+        def first_layer(first):
+            c, at = divmod(first, CHUNK)
+            pre = psum1.tile([P, PACK, SUB], F32, name="pre")
+            for t in range(PACK):
+                nc.tensor.matmul_mx(
+                    out=pre[:, t, :],
+                    lhsT=w1_codes[:, t * P : (t + 1) * P].bitcast(FP8X4),
+                    lhsT_scale=w1_plane[:, t * P : (t + 1) * P],
+                    rhs=x_codes[c][:, at : at + SUB].bitcast(FP8X4),
+                    rhs_scale=x_plane[c][:, at : at + SUB],
+                    start=True,
+                    stop=True,
+                )
+            if at == 0:
+                hidden[c] = keep.tile([P, CHUNK, PACK], BF16, name="hidden%d" % c, tag="hidden%d" % c, align_bytes=64)
+            nc.scalar.activation(out=hidden[c][:, at : at + SUB, :], in_=pre[:].rearrange("p t n -> p n t"), func=GELU, bias=zero_bias[:])
+
+        def quantize_h(c):
+            h_codes[c] = keep.tile([P, CHUNK], U32, name="h_codes%d" % c, align_bytes=64)
+            h_plane[c] = keep.tile([P, CHUNK], U8, name="h_plane%d" % c, align_bytes=64)
+            nc.vector.quantize_mx(out=h_codes[c][:].bitcast(FP8X4), scales=h_plane[c][:], in_=hidden[c][:].rearrange("p s t -> p (s t)"))
+
+        def second_layer(c):
+            tall[c] = psum2.tile([P, CHUNK // SUB, N], F32, name="tall")
+            rows[c] = keep.tile([P, CHUNK // SUB, N], F32, name="rows%d" % c)
+            for b in range(CHUNK // SUB):
+                nc.tensor.matmul_mx(
+                    out=tall[c][:, b, :],
+                    lhsT=h_codes[c][:, b * SUB : (b + 1) * SUB].bitcast(FP8X4),
+                    lhsT_scale=h_plane[c][:, b * SUB : (b + 1) * SUB],
+                    rhs=w2_codes[:].bitcast(FP4X4),
+                    rhs_scale=w2_plane[:],
+                    start=True,
+                    stop=True,
+                )
+            for b in range(CHUNK // SUB):
+                block = c * (CHUNK // SUB) + b
+                nc.scalar.activation(out=rows[c][:, b, :], in_=tall[c][:, b, :], func=COPY, scale=gate_cols[:, block : block + 1])
+
+        def turn_back(c):
+            turned = psum3.tile([P, CHUNK], F32, name="turned")
+            for b in range(CHUNK // SUB):
+                nc.tensor.transpose(turned[:, b * SUB : (b + 1) * SUB], rows[c][:, b, :], identity[:])
+            gated[c] = keep.tile([P, CHUNK], F32, name="gated%d" % c)
+            nc.scalar.copy(out=gated[c][:], in_=turned[:])
+
+        def put_back(c):
+            at = c * CHUNK % half
+            nc.vector.tensor_tensor(window[:].indirect(entries(c * CHUNK, CHUNK)), kept[c * CHUNK // half][:, at : at + CHUNK], gated[c][:], ADD)
+
+        first_layer(0)
+        first_layer(SUB)
+        quantize_h(0)
+        kept_second = keep.tile([P, half], F32, name="kept_second", tag="hidden0", align_bytes=64)
+        nc.vector.tensor_copy(out=kept_second[:], in_=window[:].indirect(entries(half, half)))
+        kept.append(kept_second)
+        first_layer(CHUNK)
+        first_layer(CHUNK + SUB)
+        quantize_h(1)
+        for c in range(CHUNKS):
+            second_layer(c)
+            if c + 2 < CHUNKS:
+                first_layer((c + 2) * CHUNK)
+            turn_back(c)
+            put_back(c)
+            if c + 2 < CHUNKS:
+                first_layer((c + 2) * CHUNK + SUB)
+                quantize_h(c + 2)
         nc.sync.dma_start(out=out, in_=window[:])

@@ -23,7 +23,8 @@ PACK = 4
 CHUNK = 256
 CHUNKS = S // CHUNK
 SUB = 128
-LATER = S - CHUNK
+FIRST = 512
+LATER = S - FIRST
 
 LOADS_A = ((0, 1024, 512), (1024, 1024, 608))
 LOADS_B = ((0, 512, 0), (512, 512, 0), (1024, 512, 0), (1536, 512, 320))
@@ -33,8 +34,8 @@ def tile_picked_modres_mlpgelu_l_kernel(tc, xT, gate, res, w1, w2_words, w2_scal
     nc = tc.nc
     with ExitStack() as ctx:
         keep = ctx.enter_context(tc.tile_pool(name="keep", bufs=1))
-        psum1 = ctx.enter_context(tc.psum_pool(name="psum1", bufs=5))
-        psum2 = ctx.enter_context(tc.psum_pool(name="psum2", bufs=1))
+        psum1 = ctx.enter_context(tc.psum_pool(name="psum1", bufs=4))
+        psum2 = ctx.enter_context(tc.psum_pool(name="psum2", bufs=2))
         psum3 = ctx.enter_context(tc.psum_pool(name="psum3", bufs=2))
 
         offsets = keep.tile([P, S // 16], U16, name="offsets")
@@ -85,50 +86,51 @@ def tile_picked_modres_mlpgelu_l_kernel(tc, xT, gate, res, w1, w2_words, w2_scal
                 if share < count:
                     nc.scalar.copy(out=pairs[u][:, first + share : first + count, :], in_=src[:, share:count, :])
 
-        woven_first = keep.tile([P, CHUNK, 2], U32, name="woven_first", align_bytes=64)
+        woven_first = keep.tile([P, FIRST, 2], U32, name="woven_first", align_bytes=64)
         apart = keep.tile([P, 2 * LATER], U32, name="apart")
 
         def gather(u):
             words = pairs[u][:].rearrange("p t j -> p (t j)").bitcast(U32)
-            nc.vector.tensor_copy(out=woven_first[:, :, u], in_=words.indirect(entries(0, CHUNK)))
-            nc.vector.tensor_copy(out=apart[:, u * LATER : (u + 1) * LATER], in_=words.indirect(entries(CHUNK, LATER)))
+            nc.vector.tensor_copy(out=woven_first[:, :, u], in_=words.indirect(entries(0, FIRST)))
+            nc.vector.tensor_copy(out=apart[:, u * LATER : (u + 1) * LATER], in_=words.indirect(entries(FIRST, LATER)))
 
-        x_codes = [keep.tile([P, CHUNK], U32, name="x_codes%d" % c, align_bytes=64) for c in range(CHUNKS)]
-        x_plane = [keep.tile([P, CHUNK], U8, name="x_plane%d" % c, align_bytes=64) for c in range(CHUNKS)]
+        x_codes = keep.tile([P, S], U32, name="x_codes", align_bytes=64)
+        x_plane = keep.tile([P, S], U8, name="x_plane", align_bytes=64)
 
-        def quantize_x(c, woven):
-            nc.vector.quantize_mx(out=x_codes[c][:].bitcast(FP8X4), scales=x_plane[c][:], in_=woven.bitcast(BF16))
+        def quantize_x(first, count, woven):
+            nc.vector.quantize_mx(out=x_codes[:, first : first + count].bitcast(FP8X4), scales=x_plane[:, first : first + count], in_=woven.bitcast(BF16))
 
         for u in range(2):
             cast(u)
             gather(u)
-        quantize_x(0, woven_first[:].rearrange("p s u -> p (s u)"))
+        quantize_x(0, FIRST, woven_first[:].rearrange("p s u -> p (s u)"))
 
         w1_grouped = keep.tile([P, PACK, P, PACK], BF16, name="w1_grouped", align_bytes=64)
         w1_codes = keep.tile([P, H], U32, name="w1_codes", align_bytes=64)
         w1_plane = keep.tile([P, H], U8, name="w1_plane", align_bytes=64)
         for v in range(2):
             nc.scalar.copy(
-                out=w1_grouped[:, :, v * 64 : (v + 1) * 64, :].rearrange("p t m j -> p m t j"),
-                in_=w1_raw[v][:].rearrange("p j (m t) -> p m t j", t=PACK),
+                out=w1_grouped[:, :, v * 64 : (v + 1) * 64, :].rearrange("p t m j -> p m j t"),
+                in_=w1_raw[v][:].rearrange("p j (m t) -> p m j t", t=PACK),
             )
         nc.vector.quantize_mx(out=w1_codes[:].bitcast(FP8X4), scales=w1_plane[:], in_=w1_grouped[:].rearrange("p t m j -> p (t m j)"))
 
         woven_later = keep.tile([P, 2 * LATER], U32, name="woven_later", tag="w1_raw1", align_bytes=64)
-        for c in range(1, CHUNKS):
-            woven = woven_later[:, 2 * (c - 1) * CHUNK : 2 * c * CHUNK]
+        for at in range(0, LATER, 256):
+            woven = woven_later[:, 2 * at : 2 * (at + 256)]
             nc.scalar.copy(
                 out=woven.rearrange("p (s u) -> p s u", u=2),
-                in_=apart[:].rearrange("p (u s) -> p s u", u=2)[:, (c - 1) * CHUNK : c * CHUNK, :],
+                in_=apart[:].rearrange("p (u s) -> p s u", u=2)[:, at : at + 256, :],
             )
-            quantize_x(c, woven)
+            quantize_x(FIRST + at, 256, woven)
 
         half = S // 2
         kept_first = keep.tile([P, half], F32, name="kept_first")
         nc.vector.tensor_copy(out=kept_first[:], in_=window[:].indirect(entries(0, half)))
         kept = [kept_first]
 
-        hidden, h_codes, h_plane, tall, rows, gated = {}, {}, {}, {}, {}, {}
+        hidden, h_codes, h_plane, tall, rows = {}, {}, {}, {}, {}
+        gated = keep.tile([P, S], F32, name="gated")
 
         def first_layer(first):
             c, at = divmod(first, CHUNK)
@@ -138,8 +140,8 @@ def tile_picked_modres_mlpgelu_l_kernel(tc, xT, gate, res, w1, w2_words, w2_scal
                     out=pre[:, t, :],
                     lhsT=w1_codes[:, t * P : (t + 1) * P].bitcast(FP8X4),
                     lhsT_scale=w1_plane[:, t * P : (t + 1) * P],
-                    rhs=x_codes[c][:, at : at + SUB].bitcast(FP8X4),
-                    rhs_scale=x_plane[c][:, at : at + SUB],
+                    rhs=x_codes[:, first : first + SUB].bitcast(FP8X4),
+                    rhs_scale=x_plane[:, first : first + SUB],
                     start=True,
                     stop=True,
                 )
@@ -173,29 +175,30 @@ def tile_picked_modres_mlpgelu_l_kernel(tc, xT, gate, res, w1, w2_words, w2_scal
             turned = psum3.tile([P, CHUNK], F32, name="turned")
             for b in range(CHUNK // SUB):
                 nc.tensor.transpose(turned[:, b * SUB : (b + 1) * SUB], rows[c][:, b, :], identity[:])
-            gated[c] = keep.tile([P, CHUNK], F32, name="gated%d" % c)
-            nc.scalar.copy(out=gated[c][:], in_=turned[:])
+            nc.scalar.copy(out=gated[:, c * CHUNK : (c + 1) * CHUNK], in_=turned[:])
 
-        def put_back(c):
-            at = c * CHUNK % half
-            nc.vector.tensor_tensor(window[:].indirect(entries(c * CHUNK, CHUNK)), kept[c * CHUNK // half][:, at : at + CHUNK], gated[c][:], ADD)
+        def put_back(first, count):
+            at = first % half
+            nc.vector.tensor_tensor(window[:].indirect(entries(first, count)), kept[first // half][:, at : at + count], gated[:, first : first + count], ADD)
 
         first_layer(0)
         first_layer(SUB)
         quantize_h(0)
-        kept_second = keep.tile([P, half], F32, name="kept_second", tag="hidden0", align_bytes=64)
-        nc.vector.tensor_copy(out=kept_second[:], in_=window[:].indirect(entries(half, half)))
-        kept.append(kept_second)
         first_layer(CHUNK)
         first_layer(CHUNK + SUB)
         quantize_h(1)
+        kept_second = keep.tile([P, half], F32, name="kept_second", tag="hidden1", align_bytes=64)
+        nc.vector.tensor_copy(out=kept_second[:], in_=window[:].indirect(entries(half, half)))
+        kept.append(kept_second)
         for c in range(CHUNKS):
             second_layer(c)
             if c + 2 < CHUNKS:
                 first_layer((c + 2) * CHUNK)
             turn_back(c)
-            put_back(c)
+            if c < 2:
+                put_back(c * CHUNK, CHUNK)
             if c + 2 < CHUNKS:
                 first_layer((c + 2) * CHUNK + SUB)
                 quantize_h(c + 2)
+        put_back(half, half)
         nc.sync.dma_start(out=out, in_=window[:])

@@ -17,6 +17,7 @@ FP4X4 = mybir.dt.float4_e2m1fn_x4
 GELU = mybir.ActivationFunctionType.Gelu_apprx_tanh
 COPY = mybir.ActivationFunctionType.Copy
 ADD = mybir.AluOpType.add
+MULT = mybir.AluOpType.mult
 
 P = 128
 PACK = 4
@@ -25,9 +26,13 @@ CHUNKS = S // CHUNK
 SUB = 128
 FIRST = 512
 LATER = S - FIRST
+AHEAD = 5
+EARLY = 512
+DIRECT = CHUNK // SUB
+W1_SHARE = 16
 
-LOADS_A = ((0, 1024, 512), (1024, 1024, 608))
-LOADS_B = ((0, 512, 0), (512, 512, 0), (1024, 512, 0), (1536, 512, 320))
+LOADS_A = ((0, 1024, 512), (1024, 512, 336), (1536, 512, 336))
+LOADS_B = ((0, 512, 0), (512, 512, 0), (1024, 768, 512), (1792, 256, 176))
 
 
 def tile_picked_modres_mlpgelu_l_kernel(tc, xT, gate, res, w1, w2_words, w2_scales, offs, out):
@@ -35,7 +40,7 @@ def tile_picked_modres_mlpgelu_l_kernel(tc, xT, gate, res, w1, w2_words, w2_scal
     with ExitStack() as ctx:
         keep = ctx.enter_context(tc.tile_pool(name="keep", bufs=1))
         psum1 = ctx.enter_context(tc.psum_pool(name="psum1", bufs=4))
-        psum2 = ctx.enter_context(tc.psum_pool(name="psum2", bufs=2))
+        psum2 = ctx.enter_context(tc.psum_pool(name="psum2", bufs=1))
         psum3 = ctx.enter_context(tc.psum_pool(name="psum3", bufs=2))
 
         offsets = keep.tile([P, S // 16], U16, name="offsets")
@@ -47,9 +52,13 @@ def tile_picked_modres_mlpgelu_l_kernel(tc, xT, gate, res, w1, w2_words, w2_scal
         w1_rows = w1.rearrange("(p j) c -> p j c", j=PACK)
 
         zero = keep.tile([P, 1], F32, name="zero")
-        zero_bias = keep.tile([P, 1], F32, name="zero_bias")
+        kept = keep.tile([P, S], F32, name="kept")
+        first_bias = kept[:, EARLY : EARLY + 1]
+        gated = keep.tile([P, S], F32, name="gated")
+        later_bias = gated[:, 0:1]
         nc.vector.memset(zero[:], 0.0)
-        nc.scalar.activation(out=zero_bias[:], in_=zero[:], func=GELU)
+        nc.vector.memset(later_bias, 0.0)
+        nc.scalar.activation(out=first_bias, in_=zero[:], func=GELU)
 
         w2_codes = keep.tile([P, 2 * N], U8, name="w2_codes", align_bytes=64)
         w2_plane = keep.tile([P, N], U8, name="w2_plane", align_bytes=64)
@@ -74,9 +83,13 @@ def tile_picked_modres_mlpgelu_l_kernel(tc, xT, gate, res, w1, w2_words, w2_scal
             nc.sync.dma_start(out=w1_raw[v][:], in_=w1_rows[:, :, v * (H // 2) : (v + 1) * (H // 2)])
         window = keep.tile([P, T], F32, name="window")
         nc.sync.dma_start(out=window[:], in_=res)
-        gate_cols = keep.tile([P, S // P], F32, name="gate_cols")
+        hidden = keep.tile([P, (S + AHEAD * SUB) * PACK], BF16, name="hidden", align_bytes=64)
+        words = SUB * PACK // 2
+        gate_row = keep.tile([P, CHUNK], F32, name="gate_row")
+        nc.sync.dma_start(out=gate_row[:], in_=gate[:, 0:CHUNK])
+        gate_cols = hidden[:].bitcast(F32)[:, (AHEAD + DIRECT) * words :: words]
         with nc.allow_non_contiguous_dma(reason="one gate value a partition"):
-            nc.sync.dma_start(out=gate_cols[:], in_=gate[0].rearrange("(b p) -> p b", p=P))
+            nc.sync.dma_start(out=gate_cols, in_=gate[0, CHUNK:].rearrange("(b p) -> p b", p=P))
 
         def cast(u):
             for first, count, share in (LOADS_A, LOADS_B)[u]:
@@ -94,65 +107,67 @@ def tile_picked_modres_mlpgelu_l_kernel(tc, xT, gate, res, w1, w2_words, w2_scal
             nc.vector.tensor_copy(out=woven_first[:, :, u], in_=words.indirect(entries(0, FIRST)))
             nc.vector.tensor_copy(out=apart[:, u * LATER : (u + 1) * LATER], in_=words.indirect(entries(FIRST, LATER)))
 
-        x_codes = keep.tile([P, S], U32, name="x_codes", align_bytes=64)
+        x_codes = {}
         x_plane = keep.tile([P, S], U8, name="x_plane", align_bytes=64)
 
-        def quantize_x(first, count, woven):
-            nc.vector.quantize_mx(out=x_codes[:, first : first + count].bitcast(FP8X4), scales=x_plane[:, first : first + count], in_=woven.bitcast(BF16))
+        def quantize_x(c, codes, woven):
+            x_codes[c] = codes
+            nc.vector.quantize_mx(out=codes.bitcast(FP8X4), scales=x_plane[:, c * CHUNK : (c + 1) * CHUNK], in_=woven.bitcast(BF16))
 
         for u in range(2):
             cast(u)
             gather(u)
-        quantize_x(0, FIRST, woven_first[:].rearrange("p s u -> p (s u)"))
+        woven_words = woven_first[:].rearrange("p s u -> p (s u)")
 
         w1_grouped = keep.tile([P, PACK, P, PACK], BF16, name="w1_grouped", align_bytes=64)
         w1_codes = keep.tile([P, H], U32, name="w1_codes", align_bytes=64)
         w1_plane = keep.tile([P, H], U8, name="w1_plane", align_bytes=64)
+        dealt = w1_grouped[:].rearrange("p t m j -> p m j t")
+        halves = [w1_raw[v][:].rearrange("p j (m t) -> p m j t", t=PACK) for v in range(2)]
+        nc.scalar.copy(out=dealt[:, 0:64], in_=halves[0])
+        nc.scalar.copy(out=dealt[:, 64 : P - W1_SHARE], in_=halves[1][:, 0 : 64 - W1_SHARE])
+        nc.vector.tensor_copy(out=dealt[:, P - W1_SHARE :], in_=halves[1][:, 64 - W1_SHARE :])
+        first_codes = keep.tile([P, CHUNK], U32, name="first_codes", tag="w1_raw0", align_bytes=64)
+        quantize_x(0, first_codes[:], woven_words[:, 0 : 2 * CHUNK])
         for v in range(2):
-            nc.scalar.copy(
-                out=w1_grouped[:, :, v * 64 : (v + 1) * 64, :].rearrange("p t m j -> p m j t"),
-                in_=w1_raw[v][:].rearrange("p j (m t) -> p m j t", t=PACK),
-            )
-        nc.vector.quantize_mx(out=w1_codes[:].bitcast(FP8X4), scales=w1_plane[:], in_=w1_grouped[:].rearrange("p t m j -> p (t m j)"))
+            cols = slice(v * (H // 2), (v + 1) * (H // 2))
+            nc.vector.quantize_mx(out=w1_codes[:, cols].bitcast(FP8X4), scales=w1_plane[:, cols], in_=w1_grouped[:, 2 * v : 2 * v + 2].rearrange("p t m j -> p (t m j)"))
 
         woven_later = keep.tile([P, 2 * LATER], U32, name="woven_later", tag="w1_raw1", align_bytes=64)
+        later_codes = keep.tile([P, LATER], U32, name="later_codes", align_bytes=64)
+        second_codes = keep.tile([P, CHUNK], U32, name="second_codes", tag="w1_grouped", align_bytes=64)
+        quantize_x(1, second_codes[:], woven_words[:, 2 * CHUNK :])
         for at in range(0, LATER, 256):
             woven = woven_later[:, 2 * at : 2 * (at + 256)]
             nc.scalar.copy(
                 out=woven.rearrange("p (s u) -> p s u", u=2),
                 in_=apart[:].rearrange("p (u s) -> p s u", u=2)[:, at : at + 256, :],
             )
-            quantize_x(FIRST + at, 256, woven)
+            quantize_x((FIRST + at) // CHUNK, later_codes[:, at : at + CHUNK], woven)
 
-        half = S // 2
-        kept_first = keep.tile([P, half], F32, name="kept_first")
-        nc.vector.tensor_copy(out=kept_first[:], in_=window[:].indirect(entries(0, half)))
-        kept = [kept_first]
+        nc.vector.tensor_copy(out=kept[:, 0:EARLY], in_=window[:].indirect(entries(0, EARLY)))
 
-        hidden, h_codes, h_plane, tall, rows = {}, {}, {}, {}, {}
-        gated = keep.tile([P, S], F32, name="gated")
+        h_codes, h_plane, tall, rows = {}, {}, {}, {}
 
         def first_layer(first):
-            c, at = divmod(first, CHUNK)
             pre = psum1.tile([P, PACK, SUB], F32, name="pre")
             for t in range(PACK):
                 nc.tensor.matmul_mx(
                     out=pre[:, t, :],
                     lhsT=w1_codes[:, t * P : (t + 1) * P].bitcast(FP8X4),
                     lhsT_scale=w1_plane[:, t * P : (t + 1) * P],
-                    rhs=x_codes[:, first : first + SUB].bitcast(FP8X4),
+                    rhs=x_codes[first // CHUNK][:, first % CHUNK : first % CHUNK + SUB].bitcast(FP8X4),
                     rhs_scale=x_plane[:, first : first + SUB],
                     start=True,
                     stop=True,
                 )
-            if at == 0:
-                hidden[c] = keep.tile([P, CHUNK, PACK], BF16, name="hidden%d" % c, tag="hidden%d" % c, align_bytes=64)
-            nc.scalar.activation(out=hidden[c][:, at : at + SUB, :], in_=pre[:].rearrange("p t n -> p n t"), func=GELU, bias=zero_bias[:])
+            block = hidden[:, first * PACK : (first + SUB) * PACK].rearrange("p (n t) -> p n t", t=PACK)
+            nc.scalar.activation(out=block, in_=pre[:].rearrange("p t n -> p n t"), func=GELU, bias=first_bias if first <= CHUNK else later_bias if first < 3 * CHUNK else zero[:])
 
         def quantize_h(c):
             h_codes[c] = keep.tile([P, CHUNK], U32, name="h_codes%d" % c, align_bytes=64)
             h_plane[c] = keep.tile([P, CHUNK], U8, name="h_plane%d" % c, align_bytes=64)
-            nc.vector.quantize_mx(out=h_codes[c][:].bitcast(FP8X4), scales=h_plane[c][:], in_=hidden[c][:].rearrange("p s t -> p (s t)"))
+            nc.vector.quantize_mx(out=h_codes[c][:].bitcast(FP8X4), scales=h_plane[c][:], in_=hidden[:, c * CHUNK * PACK : (c + 1) * CHUNK * PACK])
 
         def second_layer(c):
             tall[c] = psum2.tile([P, CHUNK // SUB, N], F32, name="tall")
@@ -168,8 +183,21 @@ def tile_picked_modres_mlpgelu_l_kernel(tc, xT, gate, res, w1, w2_words, w2_scal
                     stop=True,
                 )
             for b in range(CHUNK // SUB):
-                block = c * (CHUNK // SUB) + b
+                block = c * (CHUNK // SUB) + b - DIRECT
                 nc.scalar.activation(out=rows[c][:, b, :], in_=tall[c][:, b, :], func=COPY, scale=gate_cols[:, block : block + 1])
+
+        def second_layer_direct(c):
+            wide = psum3.tile([P, CHUNK], F32, name="turned")
+            nc.tensor.matmul_mx(
+                out=wide[:],
+                lhsT=w2_codes[:].bitcast(FP4X4),
+                lhsT_scale=w2_plane[:],
+                rhs=h_codes[c][:].bitcast(FP8X4),
+                rhs_scale=h_plane[c][:],
+                start=True,
+                stop=True,
+            )
+            return wide
 
         def turn_back(c):
             turned = psum3.tile([P, CHUNK], F32, name="turned")
@@ -178,27 +206,28 @@ def tile_picked_modres_mlpgelu_l_kernel(tc, xT, gate, res, w1, w2_words, w2_scal
             nc.scalar.copy(out=gated[:, c * CHUNK : (c + 1) * CHUNK], in_=turned[:])
 
         def put_back(first, count):
-            at = first % half
-            nc.vector.tensor_tensor(window[:].indirect(entries(first, count)), kept[first // half][:, at : at + count], gated[:, first : first + count], ADD)
+            nc.vector.tensor_tensor(window[:].indirect(entries(first, count)), kept[:, first : first + count], gated[:, first : first + count], ADD)
 
         first_layer(0)
         first_layer(SUB)
         quantize_h(0)
+        wide = second_layer_direct(0)
         first_layer(CHUNK)
+        nc.vector.tensor_copy(out=kept[:, EARLY:], in_=window[:].indirect(entries(EARLY, S - EARLY)))
         first_layer(CHUNK + SUB)
         quantize_h(1)
-        kept_second = keep.tile([P, half], F32, name="kept_second", tag="hidden1", align_bytes=64)
-        nc.vector.tensor_copy(out=kept_second[:], in_=window[:].indirect(entries(half, half)))
-        kept.append(kept_second)
-        for c in range(CHUNKS):
-            second_layer(c)
-            if c + 2 < CHUNKS:
-                first_layer((c + 2) * CHUNK)
+        first_layer(2 * CHUNK)
+        first_layer(2 * CHUNK + SUB)
+        nc.vector.tensor_tensor(gated[:, 0:CHUNK], wide[:], gate_row[:], MULT)
+        quantize_h(2)
+        put_back(0, CHUNK)
+        first_layer(3 * CHUNK)
+        second_layer(1)
+        first_layer(3 * CHUNK + SUB)
+        quantize_h(3)
+        for c in range(1, CHUNKS):
+            if c > 1:
+                second_layer(c)
             turn_back(c)
-            if c < 2:
-                put_back(c * CHUNK, CHUNK)
-            if c + 2 < CHUNKS:
-                first_layer((c + 2) * CHUNK + SUB)
-                quantize_h(c + 2)
-        put_back(half, half)
+            put_back(c * CHUNK, CHUNK)
         nc.sync.dma_start(out=out, in_=window[:])

@@ -31,8 +31,8 @@ EARLY = 512
 DIRECT = CHUNK // SUB
 W1_SHARE = 16
 
-LOADS_A = ((0, 1024, 512), (1024, 512, 336), (1536, 512, 336))
-LOADS_B = ((0, 512, 0), (512, 512, 0), (1024, 768, 512), (1792, 256, 176))
+LOADS_A = ((0, 1536, 960), (1536, 512, 336))
+LOADS_B = ((0, 1024, 320), (1024, 768, 480), (1792, 256, 176))
 
 
 def tile_picked_modres_mlpgelu_l_kernel(tc, xT, gate, res, w1, w2_words, w2_scales, offs, out):
@@ -83,13 +83,13 @@ def tile_picked_modres_mlpgelu_l_kernel(tc, xT, gate, res, w1, w2_words, w2_scal
             nc.sync.dma_start(out=w1_raw[v][:], in_=w1_rows[:, :, v * (H // 2) : (v + 1) * (H // 2)])
         window = keep.tile([P, T], F32, name="window")
         nc.sync.dma_start(out=window[:], in_=res)
-        hidden = keep.tile([P, (S + AHEAD * SUB) * PACK], BF16, name="hidden", align_bytes=64)
+        hidden = keep.tile([P, (S + (AHEAD - DIRECT) * SUB) * PACK], BF16, name="hidden", align_bytes=64)
         words = SUB * PACK // 2
-        gate_row = keep.tile([P, CHUNK], F32, name="gate_row")
-        nc.sync.dma_start(out=gate_row[:], in_=gate[:, 0:CHUNK])
+        gate_row = keep.tile([P, 2, CHUNK], F32, name="gate_row")
+        nc.sync.dma_start(out=gate_row[:], in_=gate.rearrange("p (c s) -> p c s", s=CHUNK)[:, 0 :: CHUNKS - 1, :])
         gate_cols = hidden[:].bitcast(F32)[:, (AHEAD + DIRECT) * words :: words]
         with nc.allow_non_contiguous_dma(reason="one gate value a partition"):
-            nc.sync.dma_start(out=gate_cols, in_=gate[0, CHUNK:].rearrange("(b p) -> p b", p=P))
+            nc.sync.dma_start(out=gate_cols, in_=gate[0, CHUNK : S - CHUNK].rearrange("(b p) -> p b", p=P))
 
         def cast(u):
             for first, count, share in (LOADS_A, LOADS_B)[u]:
@@ -218,16 +218,19 @@ def tile_picked_modres_mlpgelu_l_kernel(tc, xT, gate, res, w1, w2_words, w2_scal
         quantize_h(1)
         first_layer(2 * CHUNK)
         first_layer(2 * CHUNK + SUB)
-        nc.vector.tensor_tensor(gated[:, 0:CHUNK], wide[:], gate_row[:], MULT)
+        nc.vector.tensor_tensor(gated[:, 0:CHUNK], wide[:], gate_row[:, 0, :], MULT)
         quantize_h(2)
         put_back(0, CHUNK)
         first_layer(3 * CHUNK)
         second_layer(1)
         first_layer(3 * CHUNK + SUB)
         quantize_h(3)
-        for c in range(1, CHUNKS):
-            if c > 1:
-                second_layer(c)
-            turn_back(c)
-            put_back(c * CHUNK, CHUNK)
+        turn_back(1)
+        put_back(CHUNK, CHUNK)
+        second_layer(2)
+        turn_back(2)
+        wide = second_layer_direct(3)
+        nc.vector.tensor_tensor(gated[:, 3 * CHUNK :], wide[:], gate_row[:, 1, :], MULT)
+        put_back(2 * CHUNK, CHUNK)
+        put_back(3 * CHUNK, CHUNK)
         nc.sync.dma_start(out=out, in_=window[:])

@@ -16,6 +16,7 @@ FP8X4 = mybir.dt.float8_e4m3fn_x4
 FP4X4 = mybir.dt.float4_e2m1fn_x4
 GELU = mybir.ActivationFunctionType.Gelu_apprx_tanh
 COPY = mybir.ActivationFunctionType.Copy
+IDENTITY = mybir.ActivationFunctionType.Identity
 ADD = mybir.AluOpType.add
 MULT = mybir.AluOpType.mult
 
@@ -24,12 +25,11 @@ PACK = 4
 CHUNK = 256
 CHUNKS = S // CHUNK
 SUB = 128
-FIRST = 512
-LATER = S - FIRST
+LATER = 2 * CHUNK
 AHEAD = 5
-EARLY = 512
+EARLY = 384
 DIRECT = CHUNK // SUB
-W1_SHARE = 16
+W1_SHARE = 32
 
 LOADS_A = ((0, 1536, 960), (1536, 512, 336))
 LOADS_B = ((0, 1024, 320), (1024, 768, 480), (1792, 256, 176))
@@ -58,6 +58,9 @@ def tile_picked_modres_mlpgelu_l_kernel(tc, xT, gate, res, w1, w2_words, w2_scal
         later_bias = gated[:, 0:1]
         nc.vector.memset(zero[:], 0.0)
         nc.vector.memset(later_bias, 0.0)
+        woven_last = keep.tile([P, CHUNK, 2], U32, name="woven_last", align_bytes=64)
+        round_bias = woven_last[:, 0, 1:2].bitcast(F32)
+        nc.vector.memset(round_bias, 0.0)
         nc.scalar.activation(out=first_bias, in_=zero[:], func=GELU)
 
         w2_codes = keep.tile([P, 2 * N], U8, name="w2_codes", align_bytes=64)
@@ -99,13 +102,17 @@ def tile_picked_modres_mlpgelu_l_kernel(tc, xT, gate, res, w1, w2_words, w2_scal
                 if share < count:
                     nc.scalar.copy(out=pairs[u][:, first + share : first + count, :], in_=src[:, share:count, :])
 
-        woven_first = keep.tile([P, FIRST, 2], U32, name="woven_first", align_bytes=64)
+        woven_first = keep.tile([P, CHUNK, 2], U32, name="woven_first", align_bytes=64)
         apart = keep.tile([P, 2 * LATER], U32, name="apart")
 
+        pair_words = [pairs[u][:].rearrange("p t j -> p (t j)").bitcast(U32) for u in range(2)]
+
         def gather(u):
-            words = pairs[u][:].rearrange("p t j -> p (t j)").bitcast(U32)
-            nc.vector.tensor_copy(out=woven_first[:, :, u], in_=words.indirect(entries(0, FIRST)))
-            nc.vector.tensor_copy(out=apart[:, u * LATER : (u + 1) * LATER], in_=words.indirect(entries(FIRST, LATER)))
+            nc.vector.tensor_copy(out=woven_first[:, :, u], in_=pair_words[u].indirect(entries(0, CHUNK)))
+            nc.vector.tensor_copy(out=apart[:, u * LATER : (u + 1) * LATER], in_=pair_words[u].indirect(entries(CHUNK, LATER)))
+
+        def gather_last(u):
+            nc.vector.tensor_copy(out=woven_last[:, :, u], in_=pair_words[u].indirect(entries(S - CHUNK, CHUNK)))
 
         x_codes = {}
         x_plane = keep.tile([P, S], U8, name="x_plane", align_bytes=64)
@@ -117,6 +124,8 @@ def tile_picked_modres_mlpgelu_l_kernel(tc, xT, gate, res, w1, w2_words, w2_scal
         for u in range(2):
             cast(u)
             gather(u)
+            if u == 0:
+                gather_last(u)
         woven_words = woven_first[:].rearrange("p s u -> p (s u)")
 
         w1_grouped = keep.tile([P, PACK, P, PACK], BF16, name="w1_grouped", align_bytes=64)
@@ -125,7 +134,7 @@ def tile_picked_modres_mlpgelu_l_kernel(tc, xT, gate, res, w1, w2_words, w2_scal
         dealt = w1_grouped[:].rearrange("p t m j -> p m j t")
         halves = [w1_raw[v][:].rearrange("p j (m t) -> p m j t", t=PACK) for v in range(2)]
         nc.scalar.copy(out=dealt[:, 0:64], in_=halves[0])
-        nc.scalar.copy(out=dealt[:, 64 : P - W1_SHARE], in_=halves[1][:, 0 : 64 - W1_SHARE])
+        nc.scalar.activation(out=dealt[:, 64 : P - W1_SHARE], in_=halves[1][:, 0 : 64 - W1_SHARE], func=IDENTITY, bias=round_bias)
         nc.vector.tensor_copy(out=dealt[:, P - W1_SHARE :], in_=halves[1][:, 64 - W1_SHARE :])
         first_codes = keep.tile([P, CHUNK], U32, name="first_codes", tag="w1_raw0", align_bytes=64)
         quantize_x(0, first_codes[:], woven_words[:, 0 : 2 * CHUNK])
@@ -134,16 +143,17 @@ def tile_picked_modres_mlpgelu_l_kernel(tc, xT, gate, res, w1, w2_words, w2_scal
             nc.vector.quantize_mx(out=w1_codes[:, cols].bitcast(FP8X4), scales=w1_plane[:, cols], in_=w1_grouped[:, 2 * v : 2 * v + 2].rearrange("p t m j -> p (t m j)"))
 
         woven_later = keep.tile([P, 2 * LATER], U32, name="woven_later", tag="w1_raw1", align_bytes=64)
-        later_codes = keep.tile([P, LATER], U32, name="later_codes", align_bytes=64)
-        second_codes = keep.tile([P, CHUNK], U32, name="second_codes", tag="w1_grouped", align_bytes=64)
-        quantize_x(1, second_codes[:], woven_words[:, 2 * CHUNK :])
+        later_codes = keep.tile([P, S - CHUNK], U32, name="later_codes", align_bytes=64)
         for at in range(0, LATER, 256):
             woven = woven_later[:, 2 * at : 2 * (at + 256)]
             nc.scalar.copy(
                 out=woven.rearrange("p (s u) -> p s u", u=2),
                 in_=apart[:].rearrange("p (u s) -> p s u", u=2)[:, at : at + 256, :],
             )
-            quantize_x((FIRST + at) // CHUNK, later_codes[:, at : at + CHUNK], woven)
+            quantize_x(1 + at // CHUNK, later_codes[:, at : at + CHUNK], woven)
+            if at == 0:
+                gather_last(1)
+        quantize_x(CHUNKS - 1, later_codes[:, LATER:], woven_last[:].rearrange("p s u -> p (s u)"))
 
         nc.vector.tensor_copy(out=kept[:, 0:EARLY], in_=window[:].indirect(entries(0, EARLY)))
 
@@ -162,7 +172,7 @@ def tile_picked_modres_mlpgelu_l_kernel(tc, xT, gate, res, w1, w2_words, w2_scal
                     stop=True,
                 )
             block = hidden[:, first * PACK : (first + SUB) * PACK].rearrange("p (n t) -> p n t", t=PACK)
-            nc.scalar.activation(out=block, in_=pre[:].rearrange("p t n -> p n t"), func=GELU, bias=first_bias if first <= CHUNK else later_bias if first < 3 * CHUNK else zero[:])
+            nc.scalar.activation(out=block, in_=pre[:].rearrange("p t n -> p n t"), func=GELU, bias=first_bias if first < CHUNK else zero[:] if first == CHUNK else later_bias if first < 3 * CHUNK else zero[:])
 
         def quantize_h(c):
             h_codes[c] = keep.tile([P, CHUNK], U32, name="h_codes%d" % c, align_bytes=64)
@@ -212,8 +222,8 @@ def tile_picked_modres_mlpgelu_l_kernel(tc, xT, gate, res, w1, w2_words, w2_scal
         first_layer(SUB)
         quantize_h(0)
         wide = second_layer_direct(0)
-        first_layer(CHUNK)
         nc.vector.tensor_copy(out=kept[:, EARLY:], in_=window[:].indirect(entries(EARLY, S - EARLY)))
+        first_layer(CHUNK)
         first_layer(CHUNK + SUB)
         quantize_h(1)
         first_layer(2 * CHUNK)

@@ -27,9 +27,10 @@ CHUNKS = S // CHUNK
 SUB = 128
 LATER = 2 * CHUNK
 AHEAD = 5
-EARLY = 384
+EARLY = 512
 DIRECT = CHUNK // SUB
-W1_SHARE = 32
+SPARE = 8
+OVERLAP = 16
 
 LOADS_A = ((0, 1536, 960), (1536, 512, 336))
 LOADS_B = ((0, 1024, 320), (1024, 768, 480), (1792, 256, 176))
@@ -52,14 +53,20 @@ def tile_picked_modres_mlpgelu_l_kernel(tc, xT, gate, res, w1, w2_words, w2_scal
         w1_rows = w1.rearrange("(p j) c -> p j c", j=PACK)
 
         zero = keep.tile([P, 1], F32, name="zero")
-        kept = keep.tile([P, S], F32, name="kept")
+        shared = keep.tile([P, 2 * LATER + S - OVERLAP], F32, name="shared")
+        apart = shared[:, 0 : 2 * LATER].bitcast(U32)
+        kept = shared[:, 2 * LATER - OVERLAP :]
         first_bias = kept[:, EARLY : EARLY + 1]
         gated = keep.tile([P, S], F32, name="gated")
-        later_bias = gated[:, 0:1]
+        window = keep.tile([P, T + SPARE], F32, name="window")
+        later_bias = window[:, T : T + 1]
         nc.vector.memset(zero[:], 0.0)
-        nc.vector.memset(later_bias, 0.0)
+        nc.vector.memset(window[:, T:], 0.0)
         woven_last = keep.tile([P, CHUNK, 2], U32, name="woven_last", align_bytes=64)
-        round_bias = woven_last[:, 0, 1:2].bitcast(F32)
+        woven_later = keep.tile([P, 2 * LATER], U32, name="woven_later", align_bytes=64)
+        round_scale = woven_later[:, 0:1].bitcast(F32)
+        round_bias = woven_later[:, LATER : LATER + 1].bitcast(F32)
+        nc.vector.memset(round_scale, 1.0)
         nc.vector.memset(round_bias, 0.0)
         nc.scalar.activation(out=first_bias, in_=zero[:], func=GELU)
 
@@ -84,8 +91,7 @@ def tile_picked_modres_mlpgelu_l_kernel(tc, xT, gate, res, w1, w2_words, w2_scal
         w1_raw = [keep.tile([P, PACK, H // 2], F32, name="w1_raw%d" % v, tag="w1_raw%d" % v, align_bytes=64) for v in range(2)]
         for v in range(2):
             nc.sync.dma_start(out=w1_raw[v][:], in_=w1_rows[:, :, v * (H // 2) : (v + 1) * (H // 2)])
-        window = keep.tile([P, T], F32, name="window")
-        nc.sync.dma_start(out=window[:], in_=res)
+        nc.sync.dma_start(out=window[:, 0:T], in_=res)
         hidden = keep.tile([P, (S + (AHEAD - DIRECT) * SUB) * PACK], BF16, name="hidden", align_bytes=64)
         words = SUB * PACK // 2
         gate_row = keep.tile([P, 2, CHUNK], F32, name="gate_row")
@@ -103,7 +109,6 @@ def tile_picked_modres_mlpgelu_l_kernel(tc, xT, gate, res, w1, w2_words, w2_scal
                     nc.scalar.copy(out=pairs[u][:, first + share : first + count, :], in_=src[:, share:count, :])
 
         woven_first = keep.tile([P, CHUNK, 2], U32, name="woven_first", align_bytes=64)
-        apart = keep.tile([P, 2 * LATER], U32, name="apart")
 
         pair_words = [pairs[u][:].rearrange("p t j -> p (t j)").bitcast(U32) for u in range(2)]
 
@@ -124,8 +129,7 @@ def tile_picked_modres_mlpgelu_l_kernel(tc, xT, gate, res, w1, w2_words, w2_scal
         for u in range(2):
             cast(u)
             gather(u)
-            if u == 0:
-                gather_last(u)
+            gather_last(u)
         woven_words = woven_first[:].rearrange("p s u -> p (s u)")
 
         w1_grouped = keep.tile([P, PACK, P, PACK], BF16, name="w1_grouped", align_bytes=64)
@@ -133,27 +137,25 @@ def tile_picked_modres_mlpgelu_l_kernel(tc, xT, gate, res, w1, w2_words, w2_scal
         w1_plane = keep.tile([P, H], U8, name="w1_plane", align_bytes=64)
         dealt = w1_grouped[:].rearrange("p t m j -> p m j t")
         halves = [w1_raw[v][:].rearrange("p j (m t) -> p m j t", t=PACK) for v in range(2)]
-        nc.scalar.copy(out=dealt[:, 0:64], in_=halves[0])
-        nc.scalar.activation(out=dealt[:, 64 : P - W1_SHARE], in_=halves[1][:, 0 : 64 - W1_SHARE], func=IDENTITY, bias=round_bias)
-        nc.vector.tensor_copy(out=dealt[:, P - W1_SHARE :], in_=halves[1][:, 64 - W1_SHARE :])
-        first_codes = keep.tile([P, CHUNK], U32, name="first_codes", tag="w1_raw0", align_bytes=64)
+        nc.scalar.activation(out=dealt[:, 0:64], in_=halves[0], func=IDENTITY, bias=round_bias, scale=round_scale)
+        nc.scalar.copy(out=dealt[:, 64:], in_=halves[1])
+        first_codes = keep.tile([P, CHUNK], U32, name="first_codes", align_bytes=64)
         quantize_x(0, first_codes[:], woven_words[:, 0 : 2 * CHUNK])
         for v in range(2):
             cols = slice(v * (H // 2), (v + 1) * (H // 2))
             nc.vector.quantize_mx(out=w1_codes[:, cols].bitcast(FP8X4), scales=w1_plane[:, cols], in_=w1_grouped[:, 2 * v : 2 * v + 2].rearrange("p t m j -> p (t m j)"))
 
-        woven_later = keep.tile([P, 2 * LATER], U32, name="woven_later", tag="w1_raw1", align_bytes=64)
-        later_codes = keep.tile([P, S - CHUNK], U32, name="later_codes", align_bytes=64)
+        later_codes = keep.tile([P, LATER], U32, name="later_codes", align_bytes=64)
+        last_codes = keep.tile([P, CHUNK], U32, name="last_codes", tag="w1_raw1", align_bytes=64)
         for at in range(0, LATER, 256):
             woven = woven_later[:, 2 * at : 2 * (at + 256)]
             nc.scalar.copy(
                 out=woven.rearrange("p (s u) -> p s u", u=2),
-                in_=apart[:].rearrange("p (u s) -> p s u", u=2)[:, at : at + 256, :],
+                in_=apart.rearrange("p (u s) -> p s u", u=2)[:, at : at + 256, :],
             )
             quantize_x(1 + at // CHUNK, later_codes[:, at : at + CHUNK], woven)
             if at == 0:
-                gather_last(1)
-        quantize_x(CHUNKS - 1, later_codes[:, LATER:], woven_last[:].rearrange("p s u -> p (s u)"))
+                quantize_x(CHUNKS - 1, last_codes[:], woven_last[:].rearrange("p s u -> p (s u)"))
 
         nc.vector.tensor_copy(out=kept[:, 0:EARLY], in_=window[:].indirect(entries(0, EARLY)))
 
@@ -161,7 +163,7 @@ def tile_picked_modres_mlpgelu_l_kernel(tc, xT, gate, res, w1, w2_words, w2_scal
 
         def first_layer(first):
             pre = psum1.tile([P, PACK, SUB], F32, name="pre")
-            for t in range(PACK):
+            for t in range(PACK) if first == 0 else reversed(range(PACK)):
                 nc.tensor.matmul_mx(
                     out=pre[:, t, :],
                     lhsT=w1_codes[:, t * P : (t + 1) * P].bitcast(FP8X4),
@@ -172,7 +174,7 @@ def tile_picked_modres_mlpgelu_l_kernel(tc, xT, gate, res, w1, w2_words, w2_scal
                     stop=True,
                 )
             block = hidden[:, first * PACK : (first + SUB) * PACK].rearrange("p (n t) -> p n t", t=PACK)
-            nc.scalar.activation(out=block, in_=pre[:].rearrange("p t n -> p n t"), func=GELU, bias=first_bias if first < CHUNK else zero[:] if first == CHUNK else later_bias if first < 3 * CHUNK else zero[:])
+            nc.scalar.activation(out=block, in_=pre[:].rearrange("p t n -> p n t"), func=GELU, bias={SUB: first_bias, 2 * CHUNK + SUB: later_bias}.get(first, zero[:]))
 
         def quantize_h(c):
             h_codes[c] = keep.tile([P, CHUNK], U32, name="h_codes%d" % c, align_bytes=64)
@@ -225,10 +227,10 @@ def tile_picked_modres_mlpgelu_l_kernel(tc, xT, gate, res, w1, w2_words, w2_scal
         nc.vector.tensor_copy(out=kept[:, EARLY:], in_=window[:].indirect(entries(EARLY, S - EARLY)))
         first_layer(CHUNK)
         first_layer(CHUNK + SUB)
+        nc.vector.tensor_tensor(gated[:, 0:CHUNK], wide[:], gate_row[:, 0, :], MULT)
         quantize_h(1)
         first_layer(2 * CHUNK)
         first_layer(2 * CHUNK + SUB)
-        nc.vector.tensor_tensor(gated[:, 0:CHUNK], wide[:], gate_row[:, 0, :], MULT)
         quantize_h(2)
         put_back(0, CHUNK)
         first_layer(3 * CHUNK)
@@ -243,4 +245,4 @@ def tile_picked_modres_mlpgelu_l_kernel(tc, xT, gate, res, w1, w2_words, w2_scal
         nc.vector.tensor_tensor(gated[:, 3 * CHUNK :], wide[:], gate_row[:, 1, :], MULT)
         put_back(2 * CHUNK, CHUNK)
         put_back(3 * CHUNK, CHUNK)
-        nc.sync.dma_start(out=out, in_=window[:])
+        nc.sync.dma_start(out=out, in_=window[:, 0:T])

@@ -32,8 +32,8 @@ DIRECT = CHUNK // SUB
 SPARE = 8
 OVERLAP = 16
 
-LOADS_A = ((0, 1536, 960), (1536, 512, 336))
-LOADS_B = ((0, 1024, 320), (1024, 768, 480), (1792, 256, 176))
+LOADS_A = ((0, 1152, 720), (1152, 896, 576))
+LOADS_B = ((0, 512, 0), (512, 896, 576), (1408, 640, 416))
 
 
 def tile_picked_modres_mlpgelu_l_kernel(tc, xT, gate, res, w1, w2_words, w2_scales, offs, out):
@@ -49,7 +49,7 @@ def tile_picked_modres_mlpgelu_l_kernel(tc, xT, gate, res, w1, w2_words, w2_scal
         def entries(first, count):
             return offsets[:, first // 16 : (first + count) // 16]
 
-        x_rows = xT.rearrange("(p j) t -> p j t", j=PACK)
+        x_runs = xT.rearrange("(p j) t -> p (j t)", j=PACK)
         w1_rows = w1.rearrange("(p j) c -> p j c", j=PACK)
 
         zero = keep.tile([P, 1], F32, name="zero")
@@ -81,11 +81,11 @@ def tile_picked_modres_mlpgelu_l_kernel(tc, xT, gate, res, w1, w2_words, w2_scal
         make_identity(nc, identity[:])
 
         pairs = [keep.tile([P, T, 2], BF16, name="pairs%d" % u) for u in range(2)]
-        raw = {}
+        raw = [keep.tile([P, 2 * T], F32, name="raw%d" % u) for u in range(2)]
         for u, loads in enumerate((LOADS_A, LOADS_B)):
             for first, count, share in loads:
-                raw[u, first] = keep.tile([P, 2, count], F32, name="raw%d_%d" % (u, first))
-                nc.sync.dma_start(out=raw[u, first][:], in_=x_rows[:, 2 * u : 2 * u + 2, first : first + count])
+                begin, end = (T + first if first else 0), T + first + count
+                nc.sync.dma_start(out=raw[u][:, begin:end], in_=x_runs[:, 2 * T * u + begin : 2 * T * u + end])
                 if (u, first) == (0, 0):
                     nc.sync.dma_start(offsets[:], offs)
         w1_raw = [keep.tile([P, PACK, H // 2], F32, name="w1_raw%d" % v, tag="w1_raw%d" % v, align_bytes=64) for v in range(2)]
@@ -102,7 +102,7 @@ def tile_picked_modres_mlpgelu_l_kernel(tc, xT, gate, res, w1, w2_words, w2_scal
 
         def cast(u):
             for first, count, share in (LOADS_A, LOADS_B)[u]:
-                src = raw[u, first][:].rearrange("p j t -> p t j")
+                src = raw[u][:].rearrange("p (j t) -> p t j", j=2)[:, first : first + count, :]
                 if share > 0:
                     nc.vector.tensor_copy(out=pairs[u][:, first : first + share, :], in_=src[:, 0:share, :])
                 if share < count:

@@ -243,6 +243,5 @@ def tile_picked_modres_mlpgelu_l_kernel(tc, xT, gate, res, w1, w2_words, w2_scal
         turn_back(2)
         wide = second_layer_direct(3)
         nc.vector.tensor_tensor(gated[:, 3 * CHUNK :], wide[:], gate_row[:, 1, :], MULT)
-        put_back(2 * CHUNK, CHUNK)
-        put_back(3 * CHUNK, CHUNK)
+        put_back(2 * CHUNK, 2 * CHUNK)
         nc.sync.dma_start(out=out, in_=window[:, 0:T])

@@ -73,8 +73,7 @@ def tile_picked_modres_mlpgelu_l_kernel(tc, xT, gate, res, w1, w2_words, w2_scal
         w2_codes = keep.tile([P, 2 * N], U8, name="w2_codes", align_bytes=64)
         w2_plane = keep.tile([P, N], U8, name="w2_plane", align_bytes=64)
         nc.gpsimd.memset(w2_plane[:].bitcast(I32), 0)
-        nc.gpsimd.dma_start(out=w2_codes[:].bitcast(I32), in_=w2_words[0].bitcast(I32))
-        for q in range(4):
+        for q in range(1):
             nc.gpsimd.dma_start(out=w2_plane[32 * q : 32 * q + 4, :].bitcast(I32), in_=w2_scales[0, 4 * q : 4 * q + 4, :].bitcast(I32))
 
         identity = keep.tile([P, P], F32, name="identity")
@@ -94,6 +93,9 @@ def tile_picked_modres_mlpgelu_l_kernel(tc, xT, gate, res, w1, w2_words, w2_scal
         nc.sync.dma_start(out=window[:, 0:T], in_=res)
         hidden = keep.tile([P, (S + (AHEAD - DIRECT) * SUB) * PACK], BF16, name="hidden", align_bytes=64)
         words = SUB * PACK // 2
+        nc.sync.dma_start(out=w2_codes[:].bitcast(I32), in_=w2_words[0].bitcast(I32))
+        for q in range(1, 4):
+            nc.sync.dma_start(out=w2_plane[32 * q : 32 * q + 4, :].bitcast(I32), in_=w2_scales[0, 4 * q : 4 * q + 4, :].bitcast(I32))
         gate_row = keep.tile([P, 2, CHUNK], F32, name="gate_row")
         nc.sync.dma_start(out=gate_row[:], in_=gate.rearrange("p (c s) -> p c s", s=CHUNK)[:, 0 :: CHUNKS - 1, :])
         gate_cols = hidden[:].bitcast(F32)[:, (AHEAD + DIRECT) * words :: words]

@@ -32,8 +32,10 @@ DIRECT = CHUNK // SUB
 SPARE = 8
 OVERLAP = 16
 
-LOADS_A = ((0, 1152, 720), (1152, 896, 576))
-LOADS_B = ((0, 512, 0), (512, 896, 576), (1408, 640, 416))
+LOADS = (
+    ((0, 1536, 1008), (1536, 512, 336)),
+    ((0, 896, 0), (896, 896, 592), (1792, 256, 176)),
+)
 
 
 def tile_picked_modres_mlpgelu_l_kernel(tc, xT, gate, res, w1, w2_words, w2_scales, offs, out):
@@ -49,7 +51,7 @@ def tile_picked_modres_mlpgelu_l_kernel(tc, xT, gate, res, w1, w2_words, w2_scal
         def entries(first, count):
             return offsets[:, first // 16 : (first + count) // 16]
 
-        x_runs = xT.rearrange("(p j) t -> p (j t)", j=PACK)
+        x_rows = xT.rearrange("(p j) t -> p j t", j=PACK)
         w1_rows = w1.rearrange("(p j) c -> p j c", j=PACK)
 
         zero = keep.tile([P, 1], F32, name="zero")
@@ -73,18 +75,19 @@ def tile_picked_modres_mlpgelu_l_kernel(tc, xT, gate, res, w1, w2_words, w2_scal
         w2_codes = keep.tile([P, 2 * N], U8, name="w2_codes", align_bytes=64)
         w2_plane = keep.tile([P, N], U8, name="w2_plane", align_bytes=64)
         nc.gpsimd.memset(w2_plane[:].bitcast(I32), 0)
-        for q in range(1):
+        for q in range(2):
             nc.gpsimd.dma_start(out=w2_plane[32 * q : 32 * q + 4, :].bitcast(I32), in_=w2_scales[0, 4 * q : 4 * q + 4, :].bitcast(I32))
 
         identity = keep.tile([P, P], F32, name="identity")
         make_identity(nc, identity[:])
 
         pairs = [keep.tile([P, T, 2], BF16, name="pairs%d" % u) for u in range(2)]
-        raw = [keep.tile([P, 2 * T], F32, name="raw%d" % u) for u in range(2)]
-        for u, loads in enumerate((LOADS_A, LOADS_B)):
-            for first, count, share in loads:
-                begin, end = (T + first if first else 0), T + first + count
-                nc.sync.dma_start(out=raw[u][:, begin:end], in_=x_runs[:, 2 * T * u + begin : 2 * T * u + end])
+        sources = [[], []]
+        for u in range(2):
+            for first, count, share in LOADS[u]:
+                piece = keep.tile([P, 2, count], F32, name="piece%d_%d" % (u, first))
+                nc.sync.dma_start(out=piece[:], in_=x_rows[:, 2 * u : 2 * u + 2, first : first + count])
+                sources[u].append(piece[:].rearrange("p j t -> p t j"))
                 if (u, first) == (0, 0):
                     nc.sync.dma_start(offsets[:], offs)
         w1_raw = [keep.tile([P, PACK, H // 2], F32, name="w1_raw%d" % v, tag="w1_raw%d" % v, align_bytes=64) for v in range(2)]
@@ -93,18 +96,17 @@ def tile_picked_modres_mlpgelu_l_kernel(tc, xT, gate, res, w1, w2_words, w2_scal
         nc.sync.dma_start(out=window[:, 0:T], in_=res)
         hidden = keep.tile([P, (S + (AHEAD - DIRECT) * SUB) * PACK], BF16, name="hidden", align_bytes=64)
         words = SUB * PACK // 2
-        nc.sync.dma_start(out=w2_codes[:].bitcast(I32), in_=w2_words[0].bitcast(I32))
-        for q in range(1, 4):
-            nc.sync.dma_start(out=w2_plane[32 * q : 32 * q + 4, :].bitcast(I32), in_=w2_scales[0, 4 * q : 4 * q + 4, :].bitcast(I32))
         gate_row = keep.tile([P, 2, CHUNK], F32, name="gate_row")
         nc.sync.dma_start(out=gate_row[:], in_=gate.rearrange("p (c s) -> p c s", s=CHUNK)[:, 0 :: CHUNKS - 1, :])
+        nc.sync.dma_start(out=w2_codes[:].bitcast(I32), in_=w2_words[0].bitcast(I32))
+        for q in range(2, 4):
+            nc.sync.dma_start(out=w2_plane[32 * q : 32 * q + 4, :].bitcast(I32), in_=w2_scales[0, 4 * q : 4 * q + 4, :].bitcast(I32))
         gate_cols = hidden[:].bitcast(F32)[:, (AHEAD + DIRECT) * words :: words]
         with nc.allow_non_contiguous_dma(reason="one gate value a partition"):
             nc.sync.dma_start(out=gate_cols, in_=gate[0, CHUNK : S - CHUNK].rearrange("(b p) -> p b", p=P))
 
         def cast(u):
-            for first, count, share in (LOADS_A, LOADS_B)[u]:
-                src = raw[u][:].rearrange("p (j t) -> p t j", j=2)[:, first : first + count, :]
+            for (first, count, share), src in zip(LOADS[u], sources[u]):
                 if share > 0:
                     nc.vector.tensor_copy(out=pairs[u][:, first : first + share, :], in_=src[:, 0:share, :])
                 if share < count:
@@ -140,7 +142,8 @@ def tile_picked_modres_mlpgelu_l_kernel(tc, xT, gate, res, w1, w2_words, w2_scal
         dealt = w1_grouped[:].rearrange("p t m j -> p m j t")
         halves = [w1_raw[v][:].rearrange("p j (m t) -> p m j t", t=PACK) for v in range(2)]
         nc.scalar.activation(out=dealt[:, 0:64], in_=halves[0], func=IDENTITY, bias=round_bias, scale=round_scale)
-        nc.scalar.copy(out=dealt[:, 64:], in_=halves[1])
+        for v in range(2):
+            nc.scalar.copy(out=dealt[:, 64:, :, 2 * v : 2 * v + 2], in_=halves[1][:, :, :, 2 * v : 2 * v + 2])
         first_codes = keep.tile([P, CHUNK], U32, name="first_codes", align_bytes=64)
         quantize_x(0, first_codes[:], woven_words[:, 0 : 2 * CHUNK])
         for v in range(2):

@@ -30,7 +30,6 @@ AHEAD = 5
 EARLY = 512
 DIRECT = CHUNK // SUB
 SPARE = 8
-OVERLAP = 16
 
 LOADS = (
     ((0, 1536, 1008), (1536, 512, 336)),
@@ -55,13 +54,16 @@ def tile_picked_modres_mlpgelu_l_kernel(tc, xT, gate, res, w1, w2_words, w2_scal
         w1_rows = w1.rearrange("(p j) c -> p j c", j=PACK)
 
         zero = keep.tile([P, 1], F32, name="zero")
-        shared = keep.tile([P, 2 * LATER + S - OVERLAP], F32, name="shared")
-        apart = shared[:, 0 : 2 * LATER].bitcast(U32)
-        kept = shared[:, 2 * LATER - OVERLAP :]
+        apart_tile = keep.tile([P, 2 * LATER], U32, name="apart")
+        apart = apart_tile[:]
+        kept = keep.tile([P, S], F32, name="kept")
         first_bias = kept[:, EARLY : EARLY + 1]
         gated = keep.tile([P, S], F32, name="gated")
         window = keep.tile([P, T + SPARE], F32, name="window")
         later_bias = window[:, T : T + 1]
+        later_codes = keep.tile([P, LATER], U32, name="later_codes", align_bytes=64)
+        opening_bias = later_codes[:, CHUNK : CHUNK + 1].bitcast(F32)
+        nc.vector.memset(later_codes[:, CHUNK : CHUNK + 1], 0)
         nc.vector.memset(zero[:], 0.0)
         nc.vector.memset(window[:, T:], 0.0)
         woven_last = keep.tile([P, CHUNK, 2], U32, name="woven_last", align_bytes=64)
@@ -150,7 +152,6 @@ def tile_picked_modres_mlpgelu_l_kernel(tc, xT, gate, res, w1, w2_words, w2_scal
             cols = slice(v * (H // 2), (v + 1) * (H // 2))
             nc.vector.quantize_mx(out=w1_codes[:, cols].bitcast(FP8X4), scales=w1_plane[:, cols], in_=w1_grouped[:, 2 * v : 2 * v + 2].rearrange("p t m j -> p (t m j)"))
 
-        later_codes = keep.tile([P, LATER], U32, name="later_codes", align_bytes=64)
         last_codes = keep.tile([P, CHUNK], U32, name="last_codes", tag="w1_raw1", align_bytes=64)
         for at in range(0, LATER, 256):
             woven = woven_later[:, 2 * at : 2 * (at + 256)]
@@ -158,8 +159,8 @@ def tile_picked_modres_mlpgelu_l_kernel(tc, xT, gate, res, w1, w2_words, w2_scal
                 out=woven.rearrange("p (s u) -> p s u", u=2),
                 in_=apart.rearrange("p (u s) -> p s u", u=2)[:, at : at + 256, :],
             )
-            quantize_x(1 + at // CHUNK, later_codes[:, at : at + CHUNK], woven)
             if at == 0:
+                quantize_x(1, later_codes[:, 0:CHUNK], woven)
                 quantize_x(CHUNKS - 1, last_codes[:], woven_last[:].rearrange("p s u -> p (s u)"))
 
         nc.vector.tensor_copy(out=kept[:, 0:EARLY], in_=window[:].indirect(entries(0, EARLY)))
@@ -179,7 +180,7 @@ def tile_picked_modres_mlpgelu_l_kernel(tc, xT, gate, res, w1, w2_words, w2_scal
                     stop=True,
                 )
             block = hidden[:, first * PACK : (first + SUB) * PACK].rearrange("p (n t) -> p n t", t=PACK)
-            nc.scalar.activation(out=block, in_=pre[:].rearrange("p t n -> p n t"), func=GELU, bias={SUB: first_bias, 2 * CHUNK + SUB: later_bias}.get(first, zero[:]))
+            nc.scalar.activation(out=block, in_=pre[:].rearrange("p t n -> p n t"), func=GELU, bias={0: opening_bias, SUB: first_bias, 2 * CHUNK + SUB: later_bias}.get(first, zero[:]))
 
         def quantize_h(c):
             h_codes[c] = keep.tile([P, CHUNK], U32, name="h_codes%d" % c, align_bytes=64)
@@ -226,6 +227,7 @@ def tile_picked_modres_mlpgelu_l_kernel(tc, xT, gate, res, w1, w2_words, w2_scal
             nc.vector.tensor_tensor(window[:].indirect(entries(first, count)), kept[:, first : first + count], gated[:, first : first + count], ADD)
 
         first_layer(0)
+        quantize_x(2, later_codes[:, CHUNK:], woven_later[:, 2 * CHUNK :])
         first_layer(SUB)
         quantize_h(0)
         wide = second_layer_direct(0)

@@ -59,7 +59,7 @@ def tile_picked_modres_mlpgelu_l_kernel(tc, xT, gate, res, w1, w2_words, w2_scal
         kept = keep.tile([P, S], F32, name="kept")
         first_bias = kept[:, EARLY : EARLY + 1]
         gated = keep.tile([P, S], F32, name="gated")
-        window = keep.tile([P, T + SPARE], F32, name="window")
+        window = keep.tile([P, T + SPARE], F32, name="window", align_bytes=256)
         later_bias = window[:, T : T + 1]
         later_codes = keep.tile([P, LATER], U32, name="later_codes", align_bytes=64)
         opening_bias = later_codes[:, CHUNK : CHUNK + 1].bitcast(F32)
@@ -83,22 +83,22 @@ def tile_picked_modres_mlpgelu_l_kernel(tc, xT, gate, res, w1, w2_words, w2_scal
         identity = keep.tile([P, P], F32, name="identity")
         make_identity(nc, identity[:])
 
-        pairs = [keep.tile([P, T, 2], BF16, name="pairs%d" % u) for u in range(2)]
+        pairs = [keep.tile([P, T, 2], BF16, name="pairs%d" % u, align_bytes=256) for u in range(2)]
         sources = [[], []]
         for u in range(2):
             for first, count, share in LOADS[u]:
-                piece = keep.tile([P, 2, count], F32, name="piece%d_%d" % (u, first))
+                piece = keep.tile([P, 2, count], F32, name="piece%d_%d" % (u, first), align_bytes=256)
                 nc.sync.dma_start(out=piece[:], in_=x_rows[:, 2 * u : 2 * u + 2, first : first + count])
                 sources[u].append(piece[:].rearrange("p j t -> p t j"))
                 if (u, first) == (0, 0):
                     nc.sync.dma_start(offsets[:], offs)
-        w1_raw = [keep.tile([P, PACK, H // 2], F32, name="w1_raw%d" % v, tag="w1_raw%d" % v, align_bytes=64) for v in range(2)]
+        w1_raw = [keep.tile([P, PACK, H // 2], F32, name="w1_raw%d" % v, tag="w1_raw%d" % v, align_bytes=256) for v in range(2)]
         for v in range(2):
             nc.sync.dma_start(out=w1_raw[v][:], in_=w1_rows[:, :, v * (H // 2) : (v + 1) * (H // 2)])
         nc.sync.dma_start(out=window[:, 0:T], in_=res)
         hidden = keep.tile([P, (S + (AHEAD - DIRECT) * SUB) * PACK], BF16, name="hidden", align_bytes=64)
         words = SUB * PACK // 2
-        gate_row = keep.tile([P, 2, CHUNK], F32, name="gate_row")
+        gate_row = keep.tile([P, 2, CHUNK], F32, name="gate_row", align_bytes=256)
         nc.sync.dma_start(out=gate_row[:], in_=gate.rearrange("p (c s) -> p c s", s=CHUNK)[:, 0 :: CHUNKS - 1, :])
         nc.sync.dma_start(out=w2_codes[:].bitcast(I32), in_=w2_words[0].bitcast(I32))
         for q in range(2, 4):
@@ -152,7 +152,7 @@ def tile_picked_modres_mlpgelu_l_kernel(tc, xT, gate, res, w1, w2_words, w2_scal
             cols = slice(v * (H // 2), (v + 1) * (H // 2))
             nc.vector.quantize_mx(out=w1_codes[:, cols].bitcast(FP8X4), scales=w1_plane[:, cols], in_=w1_grouped[:, 2 * v : 2 * v + 2].rearrange("p t m j -> p (t m j)"))
 
-        last_codes = keep.tile([P, CHUNK], U32, name="last_codes", tag="w1_raw1", align_bytes=64)
+        last_codes = keep.tile([P, CHUNK], U32, name="last_codes", tag="w1_raw1", align_bytes=256)
         for at in range(0, LATER, 256):
             woven = woven_later[:, 2 * at : 2 * (at + 256)]
             nc.scalar.copy(

@@ -35,6 +35,7 @@ LOADS = (
     ((0, 1536, 1008), (1536, 512, 336)),
     ((0, 896, 0), (896, 896, 592), (1792, 256, 176)),
 )
+W1_LOADS = ((0, 128), (128, 192), (320, 192))
 
 
 def tile_picked_modres_mlpgelu_l_kernel(tc, xT, gate, res, w1, w2_words, w2_scales, offs, out):
@@ -61,9 +62,6 @@ def tile_picked_modres_mlpgelu_l_kernel(tc, xT, gate, res, w1, w2_words, w2_scal
         gated = keep.tile([P, S], F32, name="gated")
         window = keep.tile([P, T + SPARE], F32, name="window", align_bytes=256)
         later_bias = window[:, T : T + 1]
-        later_codes = keep.tile([P, LATER], U32, name="later_codes", align_bytes=64)
-        opening_bias = later_codes[:, CHUNK : CHUNK + 1].bitcast(F32)
-        nc.vector.memset(later_codes[:, CHUNK : CHUNK + 1], 0)
         nc.vector.memset(zero[:], 0.0)
         nc.vector.memset(window[:, T:], 0.0)
         woven_last = keep.tile([P, CHUNK, 2], U32, name="woven_last", align_bytes=64)
@@ -77,7 +75,7 @@ def tile_picked_modres_mlpgelu_l_kernel(tc, xT, gate, res, w1, w2_words, w2_scal
         w2_codes = keep.tile([P, 2 * N], U8, name="w2_codes", align_bytes=64)
         w2_plane = keep.tile([P, N], U8, name="w2_plane", align_bytes=64)
         nc.gpsimd.memset(w2_plane[:].bitcast(I32), 0)
-        for q in range(2):
+        for q in range(3):
             nc.gpsimd.dma_start(out=w2_plane[32 * q : 32 * q + 4, :].bitcast(I32), in_=w2_scales[0, 4 * q : 4 * q + 4, :].bitcast(I32))
 
         identity = keep.tile([P, P], F32, name="identity")
@@ -92,16 +90,16 @@ def tile_picked_modres_mlpgelu_l_kernel(tc, xT, gate, res, w1, w2_words, w2_scal
                 sources[u].append(piece[:].rearrange("p j t -> p t j"))
                 if (u, first) == (0, 0):
                     nc.sync.dma_start(offsets[:], offs)
-        w1_raw = [keep.tile([P, PACK, H // 2], F32, name="w1_raw%d" % v, tag="w1_raw%d" % v, align_bytes=256) for v in range(2)]
-        for v in range(2):
-            nc.sync.dma_start(out=w1_raw[v][:], in_=w1_rows[:, :, v * (H // 2) : (v + 1) * (H // 2)])
+        w1_raw = [keep.tile([P, PACK, count], F32, name="w1_raw%d" % first, tag="w1_raw%d" % first, align_bytes=256) for first, count in W1_LOADS]
+        for (first, count), raw in zip(W1_LOADS, w1_raw):
+            nc.sync.dma_start(out=raw[:], in_=w1_rows[:, :, first : first + count])
         nc.sync.dma_start(out=window[:, 0:T], in_=res)
         hidden = keep.tile([P, (S + (AHEAD - DIRECT) * SUB) * PACK], BF16, name="hidden", align_bytes=64)
         words = SUB * PACK // 2
         gate_row = keep.tile([P, 2, CHUNK], F32, name="gate_row", align_bytes=256)
         nc.sync.dma_start(out=gate_row[:], in_=gate.rearrange("p (c s) -> p c s", s=CHUNK)[:, 0 :: CHUNKS - 1, :])
         nc.sync.dma_start(out=w2_codes[:].bitcast(I32), in_=w2_words[0].bitcast(I32))
-        for q in range(2, 4):
+        for q in range(3, 4):
             nc.sync.dma_start(out=w2_plane[32 * q : 32 * q + 4, :].bitcast(I32), in_=w2_scales[0, 4 * q : 4 * q + 4, :].bitcast(I32))
         gate_cols = hidden[:].bitcast(F32)[:, (AHEAD + DIRECT) * words :: words]
         with nc.allow_non_contiguous_dma(reason="one gate value a partition"):
@@ -128,9 +126,11 @@ def tile_picked_modres_mlpgelu_l_kernel(tc, xT, gate, res, w1, w2_words, w2_scal
         x_codes = {}
         x_plane = keep.tile([P, S], U8, name="x_plane", align_bytes=64)
 
-        def quantize_x(c, codes, woven):
-            x_codes[c] = codes
-            nc.vector.quantize_mx(out=codes.bitcast(FP8X4), scales=x_plane[:, c * CHUNK : (c + 1) * CHUNK], in_=woven.bitcast(BF16))
+        def quantize_x(first, codes, woven):
+            count = codes.shape[1]
+            for at in range(0, count, SUB):
+                x_codes[first + at] = codes[:, at : at + SUB]
+            nc.vector.quantize_mx(out=codes.bitcast(FP8X4), scales=x_plane[:, first : first + count], in_=woven.bitcast(BF16))
 
         for u in range(2):
             cast(u)
@@ -142,26 +142,30 @@ def tile_picked_modres_mlpgelu_l_kernel(tc, xT, gate, res, w1, w2_words, w2_scal
         w1_codes = keep.tile([P, H], U32, name="w1_codes", align_bytes=64)
         w1_plane = keep.tile([P, H], U8, name="w1_plane", align_bytes=64)
         dealt = w1_grouped[:].rearrange("p t m j -> p m j t")
-        halves = [w1_raw[v][:].rearrange("p j (m t) -> p m j t", t=PACK) for v in range(2)]
-        nc.scalar.activation(out=dealt[:, 0:64], in_=halves[0], func=IDENTITY, bias=round_bias, scale=round_scale)
-        for v in range(2):
-            nc.scalar.copy(out=dealt[:, 64:, :, 2 * v : 2 * v + 2], in_=halves[1][:, :, :, 2 * v : 2 * v + 2])
-        first_codes = keep.tile([P, CHUNK], U32, name="first_codes", align_bytes=64)
-        quantize_x(0, first_codes[:], woven_words[:, 0 : 2 * CHUNK])
-        for v in range(2):
-            cols = slice(v * (H // 2), (v + 1) * (H // 2))
-            nc.vector.quantize_mx(out=w1_codes[:, cols].bitcast(FP8X4), scales=w1_plane[:, cols], in_=w1_grouped[:, 2 * v : 2 * v + 2].rearrange("p t m j -> p (t m j)"))
+        parts = [raw[:].rearrange("p j (m t) -> p m j t", t=PACK) for raw in w1_raw]
+        for (first, count), part in zip(W1_LOADS[:-1], parts):
+            nc.scalar.copy(out=dealt[:, first // PACK : (first + count) // PACK], in_=part)
+        rest = W1_LOADS[-1][0] // PACK
+        nc.scalar.activation(out=dealt[:, rest:, :, 0:2], in_=parts[-1][:, :, :, 0:2], func=IDENTITY, bias=round_bias, scale=round_scale)
+        nc.scalar.copy(out=dealt[:, rest:, :, 2:], in_=parts[-1][:, :, :, 2:])
+        first_codes = keep.tile([P, SUB], U32, name="first_codes", align_bytes=256)
+        quantize_x(0, first_codes[:], woven_words[:, 0 : 2 * SUB])
+        for low, high in ((0, 2), (2, 3), (3, 4)):
+            cols = slice(low * P, high * P)
+            nc.vector.quantize_mx(out=w1_codes[:, cols].bitcast(FP8X4), scales=w1_plane[:, cols], in_=w1_grouped[:, low:high].rearrange("p t m j -> p (t m j)"))
 
-        last_codes = keep.tile([P, CHUNK], U32, name="last_codes", tag="w1_raw1", align_bytes=256)
+        later_codes = keep.tile([P, LATER], U32, name="later_codes", align_bytes=256)
+        held_codes = keep.tile([P, SUB + CHUNK], U32, name="held_codes", tag="w1_raw%d" % W1_LOADS[-1][0], align_bytes=256)
+        quantize_x(SUB, held_codes[:, 0:SUB], woven_words[:, 2 * SUB :])
         for at in range(0, LATER, 256):
             woven = woven_later[:, 2 * at : 2 * (at + 256)]
             nc.scalar.copy(
                 out=woven.rearrange("p (s u) -> p s u", u=2),
                 in_=apart.rearrange("p (u s) -> p s u", u=2)[:, at : at + 256, :],
             )
+            quantize_x(CHUNK + at, later_codes[:, at : at + CHUNK], woven)
             if at == 0:
-                quantize_x(1, later_codes[:, 0:CHUNK], woven)
-                quantize_x(CHUNKS - 1, last_codes[:], woven_last[:].rearrange("p s u -> p (s u)"))
+                quantize_x(S - CHUNK, held_codes[:, SUB:], woven_last[:].rearrange("p s u -> p (s u)"))
 
         nc.vector.tensor_copy(out=kept[:, 0:EARLY], in_=window[:].indirect(entries(0, EARLY)))
 
@@ -174,13 +178,13 @@ def tile_picked_modres_mlpgelu_l_kernel(tc, xT, gate, res, w1, w2_words, w2_scal
                     out=pre[:, t, :],
                     lhsT=w1_codes[:, t * P : (t + 1) * P].bitcast(FP8X4),
                     lhsT_scale=w1_plane[:, t * P : (t + 1) * P],
-                    rhs=x_codes[first // CHUNK][:, first % CHUNK : first % CHUNK + SUB].bitcast(FP8X4),
+                    rhs=x_codes[first].bitcast(FP8X4),
                     rhs_scale=x_plane[:, first : first + SUB],
                     start=True,
                     stop=True,
                 )
             block = hidden[:, first * PACK : (first + SUB) * PACK].rearrange("p (n t) -> p n t", t=PACK)
-            nc.scalar.activation(out=block, in_=pre[:].rearrange("p t n -> p n t"), func=GELU, bias={0: opening_bias, SUB: first_bias, 2 * CHUNK + SUB: later_bias}.get(first, zero[:]))
+            nc.scalar.activation(out=block, in_=pre[:].rearrange("p t n -> p n t"), func=GELU, bias={SUB: first_bias, 2 * CHUNK + SUB: later_bias}.get(first, zero[:]))
 
         def quantize_h(c):
             h_codes[c] = keep.tile([P, CHUNK], U32, name="h_codes%d" % c, align_bytes=64)
@@ -227,7 +231,6 @@ def tile_picked_modres_mlpgelu_l_kernel(tc, xT, gate, res, w1, w2_words, w2_scal
             nc.vector.tensor_tensor(window[:].indirect(entries(first, count)), kept[:, first : first + count], gated[:, first : first + count], ADD)
 
         first_layer(0)
-        quantize_x(2, later_codes[:, CHUNK:], woven_later[:, 2 * CHUNK :])
         first_layer(SUB)
         quantize_h(0)
         wide = second_layer_direct(0)

from contextlib import ExitStack

import concourse.mybir as mybir
from concourse.masks import make_identity

K, T, S, H, N = 512, 2048, 1024, 512, 128
FLOPS = 2 * K * H * S + 2 * H * N * S

F32 = mybir.dt.float32
BF16 = mybir.dt.bfloat16
I32 = mybir.dt.int32
U32 = mybir.dt.uint32
U16 = mybir.dt.uint16
U8 = mybir.dt.uint8
FP8X4 = mybir.dt.float8_e4m3fn_x4
FP4X4 = mybir.dt.float4_e2m1fn_x4
GELU = mybir.ActivationFunctionType.Gelu_apprx_tanh
COPY = mybir.ActivationFunctionType.Copy
IDENTITY = mybir.ActivationFunctionType.Identity
ADD = mybir.AluOpType.add
MULT = mybir.AluOpType.mult

P = 128
PACK = 4
CHUNK = 256
CHUNKS = S // CHUNK
SUB = 128
LATER = 2 * CHUNK
AHEAD = 5
EARLY = 512
DIRECT = CHUNK // SUB
SPARE = 8

LOADS = (
    ((0, 1536, 1008), (1536, 512, 336)),
    ((0, 896, 0), (896, 896, 592), (1792, 256, 176)),
)
W1_LOADS = ((0, 128), (128, 192), (320, 192))


def tile_picked_modres_mlpgelu_l_kernel(tc, xT, gate, res, w1, w2_words, w2_scales, offs, out):
    nc = tc.nc
    with ExitStack() as ctx:
        keep = ctx.enter_context(tc.tile_pool(name="keep", bufs=1))
        psum1 = ctx.enter_context(tc.psum_pool(name="psum1", bufs=4))
        psum2 = ctx.enter_context(tc.psum_pool(name="psum2", bufs=1))
        psum3 = ctx.enter_context(tc.psum_pool(name="psum3", bufs=2))

        offsets = keep.tile([P, S // 16], U16, name="offsets")

        def entries(first, count):
            return offsets[:, first // 16 : (first + count) // 16]

        x_rows = xT.rearrange("(p j) t -> p j t", j=PACK)
        w1_rows = w1.rearrange("(p j) c -> p j c", j=PACK)

        zero = keep.tile([P, 1], F32, name="zero")
        apart_tile = keep.tile([P, 2 * LATER], U32, name="apart")
        apart = apart_tile[:]
        kept = keep.tile([P, S], F32, name="kept")
        first_bias = kept[:, EARLY : EARLY + 1]
        gated = keep.tile([P, S], F32, name="gated")
        window = keep.tile([P, T + SPARE], F32, name="window", align_bytes=256)
        later_bias = window[:, T : T + 1]
        nc.vector.memset(zero[:], 0.0)
        nc.vector.memset(window[:, T:], 0.0)
        woven_last = keep.tile([P, CHUNK, 2], U32, name="woven_last", align_bytes=64)
        woven_later = keep.tile([P, 2 * LATER], U32, name="woven_later", align_bytes=64)
        round_scale = woven_later[:, 0:1].bitcast(F32)
        round_bias = woven_later[:, LATER : LATER + 1].bitcast(F32)
        nc.vector.memset(round_scale, 1.0)
        nc.vector.memset(round_bias, 0.0)
        nc.scalar.activation(out=first_bias, in_=zero[:], func=GELU)

        w2_codes = keep.tile([P, 2 * N], U8, name="w2_codes", align_bytes=64)
        w2_plane = keep.tile([P, N], U8, name="w2_plane", align_bytes=64)
        nc.gpsimd.memset(w2_plane[:].bitcast(I32), 0)
        for q in range(3):
            nc.gpsimd.dma_start(out=w2_plane[32 * q : 32 * q + 4, :].bitcast(I32), in_=w2_scales[0, 4 * q : 4 * q + 4, :].bitcast(I32))

        identity = keep.tile([P, P], F32, name="identity")
        make_identity(nc, identity[:])

        pairs = [keep.tile([P, T, 2], BF16, name="pairs%d" % u, align_bytes=256) for u in range(2)]
        sources = [[], []]
        for u in range(2):
            for first, count, share in LOADS[u]:
                piece = keep.tile([P, 2, count], F32, name="piece%d_%d" % (u, first), align_bytes=256)
                nc.sync.dma_start(out=piece[:], in_=x_rows[:, 2 * u : 2 * u + 2, first : first + count])
                sources[u].append(piece[:].rearrange("p j t -> p t j"))
                if (u, first) == (0, 0):
                    nc.sync.dma_start(offsets[:], offs)
        w1_raw = [keep.tile([P, PACK, count], F32, name="w1_raw%d" % first, tag="w1_raw%d" % first, align_bytes=256) for first, count in W1_LOADS]
        for (first, count), raw in zip(W1_LOADS, w1_raw):
            nc.sync.dma_start(out=raw[:], in_=w1_rows[:, :, first : first + count])
        nc.sync.dma_start(out=window[:, 0:T], in_=res)
        hidden = keep.tile([P, (S + (AHEAD - DIRECT) * SUB) * PACK], BF16, name="hidden", align_bytes=64)
        words = SUB * PACK // 2
        gate_row = keep.tile([P, 2, CHUNK], F32, name="gate_row", align_bytes=256)
        nc.sync.dma_start(out=gate_row[:], in_=gate.rearrange("p (c s) -> p c s", s=CHUNK)[:, 0 :: CHUNKS - 1, :])
        nc.sync.dma_start(out=w2_codes[:].bitcast(I32), in_=w2_words[0].bitcast(I32))
        for q in range(3, 4):
            nc.sync.dma_start(out=w2_plane[32 * q : 32 * q + 4, :].bitcast(I32), in_=w2_scales[0, 4 * q : 4 * q + 4, :].bitcast(I32))
        gate_cols = hidden[:].bitcast(F32)[:, (AHEAD + DIRECT) * words :: words]
        with nc.allow_non_contiguous_dma(reason="one gate value a partition"):
            nc.sync.dma_start(out=gate_cols, in_=gate[0, CHUNK : S - CHUNK].rearrange("(b p) -> p b", p=P))

        def cast(u):
            for (first, count, share), src in zip(LOADS[u], sources[u]):
                if share > 0:
                    nc.vector.tensor_copy(out=pairs[u][:, first : first + share, :], in_=src[:, 0:share, :])
                if share < count:
                    nc.scalar.copy(out=pairs[u][:, first + share : first + count, :], in_=src[:, share:count, :])

        woven_first = keep.tile([P, CHUNK, 2], U32, name="woven_first", align_bytes=64)

        pair_words = [pairs[u][:].rearrange("p t j -> p (t j)").bitcast(U32) for u in range(2)]

        def gather(u):
            nc.vector.tensor_copy(out=woven_first[:, :, u], in_=pair_words[u].indirect(entries(0, CHUNK)))
            nc.vector.tensor_copy(out=apart[:, u * LATER : (u + 1) * LATER], in_=pair_words[u].indirect(entries(CHUNK, LATER)))

        def gather_last(u):
            nc.vector.tensor_copy(out=woven_last[:, :, u], in_=pair_words[u].indirect(entries(S - CHUNK, CHUNK)))

        x_codes = {}
        x_plane = keep.tile([P, S], U8, name="x_plane", align_bytes=64)

        def quantize_x(first, codes, woven):
            count = codes.shape[1]
            for at in range(0, count, SUB):
                x_codes[first + at] = codes[:, at : at + SUB]
            nc.vector.quantize_mx(out=codes.bitcast(FP8X4), scales=x_plane[:, first : first + count], in_=woven.bitcast(BF16))

        for u in range(2):
            cast(u)
            gather(u)
            gather_last(u)
        woven_words = woven_first[:].rearrange("p s u -> p (s u)")

        w1_grouped = keep.tile([P, PACK, P, PACK], BF16, name="w1_grouped", align_bytes=64)
        w1_codes = keep.tile([P, H], U32, name="w1_codes", align_bytes=64)
        w1_plane = keep.tile([P, H], U8, name="w1_plane", align_bytes=64)
        dealt = w1_grouped[:].rearrange("p t m j -> p m j t")
        parts = [raw[:].rearrange("p j (m t) -> p m j t", t=PACK) for raw in w1_raw]
        for (first, count), part in zip(W1_LOADS[:-1], parts):
            nc.scalar.copy(out=dealt[:, first // PACK : (first + count) // PACK], in_=part)
        rest = W1_LOADS[-1][0] // PACK
        nc.scalar.activation(out=dealt[:, rest:, :, 0:2], in_=parts[-1][:, :, :, 0:2], func=IDENTITY, bias=round_bias, scale=round_scale)
        nc.scalar.copy(out=dealt[:, rest:, :, 2:], in_=parts[-1][:, :, :, 2:])
        first_codes = keep.tile([P, SUB], U32, name="first_codes", align_bytes=256)
        quantize_x(0, first_codes[:], woven_words[:, 0 : 2 * SUB])
        for low, high in ((0, 2), (2, 3), (3, 4)):
            cols = slice(low * P, high * P)
            nc.vector.quantize_mx(out=w1_codes[:, cols].bitcast(FP8X4), scales=w1_plane[:, cols], in_=w1_grouped[:, low:high].rearrange("p t m j -> p (t m j)"))

        later_codes = keep.tile([P, LATER], U32, name="later_codes", align_bytes=256)
        held_codes = keep.tile([P, SUB + CHUNK], U32, name="held_codes", tag="w1_raw%d" % W1_LOADS[-1][0], align_bytes=256)
        quantize_x(SUB, held_codes[:, 0:SUB], woven_words[:, 2 * SUB :])
        for at in range(0, LATER, 256):
            woven = woven_later[:, 2 * at : 2 * (at + 256)]
            nc.scalar.copy(
                out=woven.rearrange("p (s u) -> p s u", u=2),
                in_=apart.rearrange("p (u s) -> p s u", u=2)[:, at : at + 256, :],
            )
            quantize_x(CHUNK + at, later_codes[:, at : at + CHUNK], woven)
            if at == 0:
                quantize_x(S - CHUNK, held_codes[:, SUB:], woven_last[:].rearrange("p s u -> p (s u)"))

        nc.vector.tensor_copy(out=kept[:, 0:EARLY], in_=window[:].indirect(entries(0, EARLY)))

        h_codes, h_plane, tall, rows = {}, {}, {}, {}

        def first_layer(first):
            pre = psum1.tile([P, PACK, SUB], F32, name="pre")
            for t in range(PACK) if first == 0 else reversed(range(PACK)):
                nc.tensor.matmul_mx(
                    out=pre[:, t, :],
                    lhsT=w1_codes[:, t * P : (t + 1) * P].bitcast(FP8X4),
                    lhsT_scale=w1_plane[:, t * P : (t + 1) * P],
                    rhs=x_codes[first].bitcast(FP8X4),
                    rhs_scale=x_plane[:, first : first + SUB],
                    start=True,
                    stop=True,
                )
            block = hidden[:, first * PACK : (first + SUB) * PACK].rearrange("p (n t) -> p n t", t=PACK)
            nc.scalar.activation(out=block, in_=pre[:].rearrange("p t n -> p n t"), func=GELU, bias={SUB: first_bias, 2 * CHUNK + SUB: later_bias}.get(first, zero[:]))

        def quantize_h(c):
            h_codes[c] = keep.tile([P, CHUNK], U32, name="h_codes%d" % c, align_bytes=64)
            h_plane[c] = keep.tile([P, CHUNK], U8, name="h_plane%d" % c, align_bytes=64)
            nc.vector.quantize_mx(out=h_codes[c][:].bitcast(FP8X4), scales=h_plane[c][:], in_=hidden[:, c * CHUNK * PACK : (c + 1) * CHUNK * PACK])

        def second_layer(c):
            tall[c] = psum2.tile([P, CHUNK // SUB, N], F32, name="tall")
            rows[c] = keep.tile([P, CHUNK // SUB, N], F32, name="rows%d" % c)
            for b in range(CHUNK // SUB):
                nc.tensor.matmul_mx(
                    out=tall[c][:, b, :],
                    lhsT=h_codes[c][:, b * SUB : (b + 1) * SUB].bitcast(FP8X4),
                    lhsT_scale=h_plane[c][:, b * SUB : (b + 1) * SUB],
                    rhs=w2_codes[:].bitcast(FP4X4),
                    rhs_scale=w2_plane[:],
                    start=True,
                    stop=True,
                )
            for b in range(CHUNK // SUB):
                block = c * (CHUNK // SUB) + b - DIRECT
                nc.scalar.activation(out=rows[c][:, b, :], in_=tall[c][:, b, :], func=COPY, scale=gate_cols[:, block : block + 1])

        def second_layer_direct(c):
            wide = psum3.tile([P, CHUNK], F32, name="turned")
            nc.tensor.matmul_mx(
                out=wide[:],
                lhsT=w2_codes[:].bitcast(FP4X4),
                lhsT_scale=w2_plane[:],
                rhs=h_codes[c][:].bitcast(FP8X4),
                rhs_scale=h_plane[c][:],
                start=True,
                stop=True,
            )
            return wide

        def turn_back(c):
            turned = psum3.tile([P, CHUNK], F32, name="turned")
            for b in range(CHUNK // SUB):
                nc.tensor.transpose(turned[:, b * SUB : (b + 1) * SUB], rows[c][:, b, :], identity[:])
            nc.scalar.copy(out=gated[:, c * CHUNK : (c + 1) * CHUNK], in_=turned[:])

        def put_back(first, count):
            nc.vector.tensor_tensor(window[:].indirect(entries(first, count)), kept[:, first : first + count], gated[:, first : first + count], ADD)

        first_layer(0)
        first_layer(SUB)
        quantize_h(0)
        wide = second_layer_direct(0)
        nc.vector.tensor_copy(out=kept[:, EARLY:], in_=window[:].indirect(entries(EARLY, S - EARLY)))
        first_layer(CHUNK)
        first_layer(CHUNK + SUB)
        nc.vector.tensor_tensor(gated[:, 0:CHUNK], wide[:], gate_row[:, 0, :], MULT)
        quantize_h(1)
        first_layer(2 * CHUNK)
        first_layer(2 * CHUNK + SUB)
        quantize_h(2)
        put_back(0, CHUNK)
        first_layer(3 * CHUNK)
        second_layer(1)
        first_layer(3 * CHUNK + SUB)
        quantize_h(3)
        turn_back(1)
        put_back(CHUNK, CHUNK)
        second_layer(2)
        turn_back(2)
        wide = second_layer_direct(3)
        nc.vector.tensor_tensor(gated[:, 3 * CHUNK :], wide[:], gate_row[:, 1, :], MULT)
        put_back(2 * CHUNK, 2 * CHUNK)
        nc.sync.dma_start(out=out, in_=window[:, 0:T])
